import numpy as np
import ml_dtypes


def mxq(x, axis, fmt="e4m3"):
    dtype, down = {"e4m3": (ml_dtypes.float8_e4m3fn, 7), "e5m2": (ml_dtypes.float8_e5m2, 14)}[fmt]
    v = np.moveaxis(np.asarray(x, np.float32).astype(ml_dtypes.bfloat16).astype(np.float64), axis, -1)
    blocks = v.reshape(v.shape[:-1] + (-1, 32))
    amax = np.abs(blocks).max(-1, keepdims=True)
    byte = np.maximum(np.where(amax > 0, np.frexp(amax)[1] - 1 + 127, 0) - down, 1)
    scale = np.exp2(byte - 127.0)
    codes = (blocks / scale).astype(np.float32).astype(dtype).astype(np.float64)
    return np.moveaxis((codes * scale).reshape(v.shape), -1, axis)


WIDE = False


def mx_kscale(k):
    if not WIDE:
        return np.ones(k)
    levels = np.array([10, -10, 5, -5, 0])
    if k % 512:
        return np.exp2(np.random.permutation(np.resize(levels, k // 32))).repeat(32)
    a = np.empty((k // 512, 16))
    for p in range(k // 512):
        a[p, :8] = np.random.permutation(np.resize(levels, 8))
        for g in range(8):
            far = levels[np.abs(levels - a[p, g]) >= 10]
            a[p, g + 8] = far[np.random.randint(len(far))]
    return np.exp2(a.ravel()).repeat(32)


def f64(x):
    return np.asarray(x).astype(np.float64)


def striped(idx):
    return np.tile(np.asarray(idx).reshape(-1, 16).T, (8, 1)).astype(np.uint16)


def unstriped(offs):
    return offs[:16].T.reshape(-1).astype(np.int64)


E2M1 = np.array([0.0, 0.5, 1.0, 1.5, 2.0, 3.0, 4.0, 6.0, -0.0, -0.5, -1.0, -1.5, -2.0, -3.0, -4.0, -6.0])


def pack_weight(w, fmt):
    k, n = w.shape
    w = f64(np.asarray(w, np.float32).astype(ml_dtypes.bfloat16)).reshape(k // 32, 32, n)
    amax = np.abs(w).max(1)
    if fmt == "e4m3":
        byte = np.frexp(amax)[1] - 1 + 127 - 7
    else:
        mant, ex = np.frexp(amax / 6.0)
        byte = np.where(mant > 0.5, ex, ex - 1) + 127
    byte = np.clip(np.where(amax > 0, byte, 1), 1, 254)
    scaled = (w * np.exp2(127.0 - byte)[:, None, :]).reshape(k, n).astype(np.float32)
    by_word = np.ascontiguousarray(scaled.reshape(k // 512, 128, 4, n).transpose(0, 1, 3, 2))
    if fmt == "e4m3":
        words = by_word.astype(ml_dtypes.float8_e4m3fn).view(np.uint8)
    else:
        c = by_word.astype(ml_dtypes.float4_e2m1fn).view(np.uint8) & 0xF
        words = (c[..., 0::2] | (c[..., 1::2] << 4)).reshape(k // 512, 128, 2 * n)
    return np.ascontiguousarray(words), np.ascontiguousarray(byte.astype(np.uint8).reshape(k // 512, 16, n))


def unpack_weight(words, scales, fmt):
    g, _, n = scales.shape
    words = np.ascontiguousarray(words).reshape(g, 128, n, -1)
    if fmt == "e4m3":
        vals = words.view(ml_dtypes.float8_e4m3fn).astype(np.float64)
    else:
        nib = np.empty((g, 128, n, 4), np.uint8)
        nib[..., 0::2] = words & 0xF
        nib[..., 1::2] = words >> 4
        vals = E2M1[nib]
    vals = vals * np.repeat(np.exp2(scales.astype(np.float64) - 127.0), 8, axis=1)[..., None]
    return vals.transpose(0, 1, 3, 2).reshape(g * 512, n)


def bf(x):
    return np.asarray(x, np.float32).astype(ml_dtypes.bfloat16)


def planes(Y):
    r, m = Y.shape
    b = f64(bf(Y)).reshape(r // 32, 32, m)
    amax = np.abs(b).max(1)
    byte = np.clip(np.where(amax > 0, np.frexp(amax)[1] - 1 + 127 - 7, 1), 1, 254)
    codes = (b * np.exp2(127.0 - byte)[:, None, :]).reshape(r, m).astype(np.float32).astype(ml_dtypes.float8_e4m3fn).view(np.uint8)
    words = codes.reshape(r // 512, 128, 4, m).transpose(0, 1, 3, 2)
    return np.ascontiguousarray(words), np.ascontiguousarray(byte.astype(np.uint8).reshape(r // 512, 16, m))


B, N, T, D, NQ = 1, 512, 2048, 512, 512


def setup_inputs():
    n = np.random.standard_normal
    idx = np.random.permutation(T)[:B * N]
    s = mx_kscale(D)[:, None]
    kp = pack_weight(n((D, T)) / s, "e4m3")
    return {
        "qT": (n((B, D, NQ)) * s * (2.00 / np.sqrt(D))).astype(np.float32),
        "k_words": kp[0],
        "k_scales": kp[1],
        "ls": (np.random.uniform(7.8, 8.4, (B, 1, NQ))).astype(np.float32),
        "offs": striped(idx),
    }


def reference(qT, k_words, k_scales, ls, offs):
    idx = unstriped(offs)
    pick = lambda x, which: x[:, which].reshape(x.shape[0], B, -1).transpose(1, 0, 2)
    k = unpack_weight(k_words, k_scales, "e4m3")
    kg = pick(k, idx)
    qq = mxq(f64(qT), 1, "e4m3")
    a = kg.transpose(0, 2, 1) @ qq
    y = np.exp(20.0 * np.tanh(a / 20.0) - f64(ls))
    Y = y[0]
    words, scales = planes(Y)
    return Y, words, scales

@@ -1,0 +1,167 @@
+from contextlib import ExitStack
+
+import concourse.mybir as mybir
+
+N, T, D, NQ = 512, 2048, 512, 512
+FLOPS = 2 * N * D * NQ
+
+F32 = mybir.dt.float32
+BF16 = mybir.dt.bfloat16
+I32 = mybir.dt.int32
+U32 = mybir.dt.uint32
+U16 = mybir.dt.uint16
+U8 = mybir.dt.uint8
+FP8X4 = mybir.dt.float8_e4m3fn_x4
+ACT = mybir.ActivationFunctionType
+ALU = mybir.AluOpType
+
+P = 128
+PACK = 4
+QC = 128
+CHUNKS = NQ // QC
+CAP = 20.0
+
+
+def tile_attend_plw_cap_topk_kernel(tc, qT, k_words, k_scales, ls, offs, out_0, out_1, out_2):
+    nc = tc.nc
+    with ExitStack() as ctx:
+        sb = ctx.enter_context(tc.tile_pool(name="sb", bufs=1))
+        late = ctx.enter_context(tc.tile_pool(name="late", bufs=1))
+        ps = ctx.enter_context(tc.psum_pool(name="ps", bufs=1))
+
+        offsets = sb.tile([P, N // 16], U16, name="offsets")
+        nc.sync.dma_start(offsets[:], offs)
+
+        ls_cols = sb.tile([P, PACK], F32, name="ls_cols")
+        nc.scalar.dma_start(ls_cols[:], ls[0, 0, :].rearrange("(n m) -> n m", m=PACK))
+
+        q_rows = qT[0].rearrange("(p j) q -> p j q", j=PACK)
+        q_first = sb.tile([P, PACK, QC], F32, name="q_raw0")
+        nc.sync.dma_start(q_first[:], q_rows[:, :, 0:QC])
+        q_raw = [q_first]
+
+        blank = late.tile([P, T + (CHUNKS - 1) * PACK * QC], F32, name="blank", offset=0)
+        nc.vector.memset(blank[:, 0:P], 0.0)
+        pool_scales = sb.tile([P, T], U8, name="pool_scales", align_bytes=64)
+        nc.vector.memset(pool_scales[:].bitcast(I32), 0)
+        for quad in range(4):
+            queue = nc.sync if quad % 2 == 0 else nc.scalar
+            queue.dma_start(
+                pool_scales[32 * quad : 32 * quad + 4, :].bitcast(I32),
+                k_scales[0, 4 * quad : 4 * quad + 4, :].bitcast(I32),
+            )
+
+        identity = sb.tile([P, P], F32, name="identity")
+        nc.gpsimd.affine_select(
+            out=identity[:],
+            in_=blank[:, 0:P],
+            pattern=[[-1, P]],
+            compare_op=ALU.not_equal,
+            fill=1.0,
+            base=0,
+            channel_multiplier=1,
+        )
+
+        pool_words = late.tile([P, T], U32, name="pool_words", offset=0)
+        nc.sync.dma_start(
+            pool_words[:].bitcast(I32),
+            k_words[0].rearrange("p t r -> p (t r)").bitcast(I32),
+        )
+
+        for c in range(1, CHUNKS):
+            raw = late.tile([P, PACK, QC], F32, name="q_raw%d" % c, offset=4 * (T + (c - 1) * PACK * QC))
+            nc.sync.dma_start(raw[:], q_rows[:, :, c * QC : (c + 1) * QC])
+            q_raw.append(raw)
+
+        listed_scales = sb.tile([P, N], U8, name="listed_scales", align_bytes=64)
+        nc.vector.tensor_copy(listed_scales[:], pool_scales[:].indirect(offsets[:]))
+        key_scales = sb.tile([P, N], U8, name="key_scales", align_bytes=64)
+        nc.vector.tensor_copy(
+            key_scales[:].rearrange("p (r s) -> p r s", r=PACK),
+            listed_scales[:].rearrange("p (s r) -> p r s", r=PACK),
+        )
+        key_words = sb.tile([P, N], U32, name="key_words", align_bytes=64)
+        nc.vector.tensor_copy(
+            key_words[:].rearrange("p (r s) -> p s r", r=PACK),
+            pool_words[:].indirect(offsets[:]),
+        )
+
+        ls_bank = ps.tile([P, PACK, P], F32, name="ls_bank")
+        for m in range(PACK):
+            nc.tensor.transpose(ls_bank[:, m, :], ls_cols[:, m : m + 1].to_broadcast([P, P]), identity[:])
+        ls_rows = sb.tile([P, NQ], F32, name="ls_rows")
+        nc.scalar.copy(ls_rows[:].rearrange("p (n m) -> p n m", m=PACK), ls_bank[:].rearrange("p m n -> p n m"))
+
+        scores = []
+        for c in range(CHUNKS):
+            grouped = sb.tile([P, QC, PACK], BF16, name="q_grouped%d" % c, tag="slot%d" % c, align_bytes=64)
+            if c < 2:
+                nc.scalar.copy(grouped[:], q_raw[c][:].rearrange("p j q -> p q j"))
+            else:
+                nc.vector.tensor_copy(grouped[:], q_raw[c][:].rearrange("p j q -> p q j"))
+            q_words = sb.tile([P, QC], U32, name="q_words%d" % c, align_bytes=64)
+            q_scales = sb.tile([P, QC], U8, name="q_scales%d" % c, align_bytes=64)
+            nc.vector.quantize_mx(q_words[:].bitcast(FP8X4), q_scales[:], grouped[:].rearrange("p q j -> p (q j)"))
+            bank = ps.tile([P, PACK, QC], F32, name="scores%d" % c)
+            for r in range(PACK):
+                nc.tensor.matmul_mx(
+                    out=bank[:, r, :],
+                    lhsT=key_words[:, r * P : (r + 1) * P].bitcast(FP8X4),
+                    lhsT_scale=key_scales[:, r * P : (r + 1) * P],
+                    rhs=q_words[:].bitcast(FP8X4),
+                    rhs_scale=q_scales[:],
+                    start=True,
+                    stop=True,
+                )
+            scores.append(bank)
+
+        y_words = sb.tile([P, NQ], U32, name="y_words", align_bytes=64)
+        y_scales = sb.tile([P, NQ], U8, name="y_scales", align_bytes=64)
+        y_rows = out_0.rearrange("(p r) q -> p r q", r=PACK)
+        words_out = out_1[0].rearrange("p q u -> p (q u)").bitcast(I32)
+        logits = []
+
+        def cap(c):
+            capped = sb.tile([P, PACK, QC], F32, name="capped%d" % c)
+            nc.scalar.activation(capped[:], scores[c][:], ACT.Tanh, scale=1.0 / CAP)
+            logit = sb.tile([P, PACK, QC], F32, name="logit%d" % c, tag="slot%d" % (CHUNKS - 1 - c), align_bytes=64)
+            nc.vector.scalar_tensor_tensor(
+                logit[:],
+                capped[:],
+                CAP,
+                ls_rows[:, c * QC : (c + 1) * QC].unsqueeze(1).to_broadcast([P, PACK, QC]),
+                ALU.mult,
+                ALU.subtract,
+            )
+            logits.append(logit)
+
+        def weigh(c, pieces):
+            y = sb.tile([P, PACK, QC], F32, name="y%d" % c)
+            width = QC // pieces
+            for piece in range(pieces):
+                part = slice(piece * width, (piece + 1) * width)
+                cols = slice(c * QC + piece * width, c * QC + (piece + 1) * width)
+                nc.scalar.activation(y[:, :, part], logits[c][:, :, part], ACT.Exp)
+                grouped = sb.tile([P, width, PACK], BF16, name="y_grouped%d_%d" % (c, piece), align_bytes=64)
+                nc.vector.tensor_copy(grouped[:], y[:, :, part].rearrange("p r q -> p q r"))
+                nc.vector.quantize_mx(
+                    y_words[:, cols].bitcast(FP8X4), y_scales[:, cols], grouped[:].rearrange("p q r -> p (q r)")
+                )
+            nc.sync.dma_start(y_rows[:, :, c * QC : (c + 1) * QC], y[:])
+
+        cap(0)
+        cap(1)
+        cap(2)
+        weigh(0, 1)
+        cap(3)
+        weigh(1, 1)
+        weigh(2, 1)
+        nc.sync.dma_start(words_out[:, 0 : 3 * QC], y_words[:, 0 : 3 * QC].bitcast(I32))
+        weigh(3, 2)
+        nc.sync.dma_start(words_out[:, 3 * QC :], y_words[:, 3 * QC :].bitcast(I32))
+        for quad in range(4):
+            queue = nc.sync if quad == 0 else nc.scalar
+            queue.dma_start(
+                out_2[0, 4 * quad : 4 * quad + 4, :].bitcast(I32),
+                y_scales[32 * quad : 32 * quad + 4, :].bitcast(I32),
+            )

@@ -119,46 +119,79 @@ def tile_attend_plw_cap_topk_kernel(tc, qT, k_words, k_scales, ls, offs, out_0, 
         y_scales = sb.tile([P, NQ], U8, name="y_scales", align_bytes=64)
         y_rows = out_0.rearrange("(p r) q -> p r q", r=PACK)
         words_out = out_1[0].rearrange("p q u -> p (q u)").bitcast(I32)
-        logits = []
+        y_grouped = sb.tile([P, NQ * PACK], BF16, name="y_grouped", align_bytes=64)
+        y = [sb.tile([P, PACK, QC], F32, name="y%d" % c) for c in range(CHUNKS)]
+        logits = {}
 
-        def cap(c):
-            capped = sb.tile([P, PACK, QC], F32, name="capped%d" % c)
-            nc.scalar.activation(capped[:], scores[c][:], ACT.Tanh, scale=1.0 / CAP)
-            logit = sb.tile([P, PACK, QC], F32, name="logit%d" % c, tag="slot%d" % (CHUNKS - 1 - c), align_bytes=64)
+        def cap(first, width):
+            c, part = first // QC, slice(first % QC, first % QC + width)
+            capped = sb.tile([P, PACK, width], F32, name="capped%d" % first)
+            nc.scalar.activation(capped[:], scores[c][:, :, part], ACT.Tanh, scale=1.0 / CAP)
+            if first == 0:
+                logits[first] = late.tile([P, PACK, width], F32, name="logit0", offset=4 * (T + 2 * PACK * QC))
+            else:
+                logits[first] = sb.tile(
+                    [P, PACK, width], F32, name="logit%d" % first, tag="slot%d" % (len(logits) + 2), align_bytes=64
+                )
             nc.vector.scalar_tensor_tensor(
-                logit[:],
+                logits[first][:],
                 capped[:],
                 CAP,
-                ls_rows[:, c * QC : (c + 1) * QC].unsqueeze(1).to_broadcast([P, PACK, QC]),
+                ls_rows[:, first : first + width].unsqueeze(1).to_broadcast([P, PACK, width]),
                 ALU.mult,
                 ALU.subtract,
             )
-            logits.append(logit)
 
-        def weigh(c, pieces):
-            y = sb.tile([P, PACK, QC], F32, name="y%d" % c)
-            width = QC // pieces
-            for piece in range(pieces):
-                part = slice(piece * width, (piece + 1) * width)
-                cols = slice(c * QC + piece * width, c * QC + (piece + 1) * width)
-                nc.scalar.activation(y[:, :, part], logits[c][:, :, part], ACT.Exp)
-                grouped = sb.tile([P, width, PACK], BF16, name="y_grouped%d_%d" % (c, piece), align_bytes=64)
-                nc.vector.tensor_copy(grouped[:], y[:, :, part].rearrange("p r q -> p q r"))
-                nc.vector.quantize_mx(
-                    y_words[:, cols].bitcast(FP8X4), y_scales[:, cols], grouped[:].rearrange("p q r -> p (q r)")
-                )
-            nc.sync.dma_start(y_rows[:, :, c * QC : (c + 1) * QC], y[:])
+        def group_cols(first, width):
+            return y_grouped[:, first * PACK : (first + width) * PACK]
 
-        cap(0)
-        cap(1)
-        cap(2)
-        weigh(0, 1)
-        cap(3)
-        weigh(1, 1)
-        weigh(2, 1)
-        nc.sync.dma_start(words_out[:, 0 : 3 * QC], y_words[:, 0 : 3 * QC].bitcast(I32))
-        weigh(3, 2)
-        nc.sync.dma_start(words_out[:, 3 * QC :], y_words[:, 3 * QC :].bitcast(I32))
+        def weigh(first, width):
+            c, part = first // QC, slice(first % QC, first % QC + width)
+            nc.scalar.activation(y[c][:, :, part], logits[first][:], ACT.Exp)
+
+        def group(first, width):
+            c, part = first // QC, slice(first % QC, first % QC + width)
+            nc.vector.tensor_copy(
+                group_cols(first, width).rearrange("p (q r) -> p q r", r=PACK),
+                y[c][:, :, part].rearrange("p r q -> p q r"),
+            )
+
+        def store(c):
+            nc.sync.dma_start(y_rows[:, :, c * QC : (c + 1) * QC], y[c][:])
+
+        def planes(first, width):
+            cols = slice(first, first + width)
+            nc.vector.quantize_mx(y_words[:, cols].bitcast(FP8X4), y_scales[:, cols], group_cols(first, width))
+
+        def store_words(first, width):
+            cols = slice(first, first + width)
+            nc.sync.dma_start(words_out[:, cols], y_words[:, cols].bitcast(I32))
+
+        tail = QC // 2
+        cap(0, QC)
+        cap(QC, QC)
+        cap(2 * QC, QC)
+        weigh(0, QC)
+        store(0)
+        weigh(QC, QC)
+        store(1)
+        cap(3 * QC, tail)
+        cap(3 * QC + tail, tail)
+        group(0, QC)
+        group(QC, QC)
+        planes(0, 2 * QC)
+        store_words(0, 2 * QC)
+        weigh(2 * QC, QC)
+        store(2)
+        group(2 * QC, QC)
+        weigh(3 * QC, tail)
+        group(3 * QC, tail)
+        weigh(3 * QC + tail, tail)
+        store(3)
+        group(3 * QC + tail, tail)
+        planes(2 * QC, QC)
+        planes(3 * QC, QC)
+        store_words(2 * QC, 2 * QC)
         for quad in range(4):
             queue = nc.sync if quad == 0 else nc.scalar
             queue.dma_start(

@@ -29,9 +29,6 @@ def tile_attend_plw_cap_topk_kernel(tc, qT, k_words, k_scales, ls, offs, out_0, 
         late = ctx.enter_context(tc.tile_pool(name="late", bufs=1))
         ps = ctx.enter_context(tc.psum_pool(name="ps", bufs=1))
 
-        offsets = sb.tile([P, N // 16], U16, name="offsets")
-        nc.sync.dma_start(offsets[:], offs)
-
         ls_cols = sb.tile([P, PACK], F32, name="ls_cols")
         nc.scalar.dma_start(ls_cols[:], ls[0, 0, :].rearrange("(n m) -> n m", m=PACK))
 
@@ -39,6 +36,9 @@ def tile_attend_plw_cap_topk_kernel(tc, qT, k_words, k_scales, ls, offs, out_0, 
         q_first = sb.tile([P, PACK, QC], F32, name="q_raw0")
         nc.sync.dma_start(q_first[:], q_rows[:, :, 0:QC])
         q_raw = [q_first]
+
+        offsets = sb.tile([P, N // 16], U16, name="offsets")
+        nc.sync.dma_start(offsets[:], offs)
 
         blank = late.tile([P, T + (CHUNKS - 1) * PACK * QC], F32, name="blank", offset=0)
         nc.vector.memset(blank[:, 0:P], 0.0)
@@ -98,7 +98,10 @@ def tile_attend_plw_cap_topk_kernel(tc, qT, k_words, k_scales, ls, offs, out_0, 
             if c < 2:
                 nc.scalar.copy(grouped[:], q_raw[c][:].rearrange("p j q -> p q j"))
             else:
-                nc.vector.tensor_copy(grouped[:], q_raw[c][:].rearrange("p j q -> p q j"))
+                nc.vector.tensor_copy(
+                    grouped[:].rearrange("p (g i) j -> p g j i", i=4),
+                    q_raw[c][:].rearrange("p j (g i) -> p g j i", i=4),
+                )
             q_words = sb.tile([P, QC], U32, name="q_words%d" % c, align_bytes=64)
             q_scales = sb.tile([P, QC], U8, name="q_scales%d" % c, align_bytes=64)
             nc.vector.quantize_mx(q_words[:].bitcast(FP8X4), q_scales[:], grouped[:].rearrange("p q j -> p (q j)"))
@@ -152,8 +155,8 @@ def tile_attend_plw_cap_topk_kernel(tc, qT, k_words, k_scales, ls, offs, out_0, 
         def group(first, width):
             c, part = first // QC, slice(first % QC, first % QC + width)
             nc.vector.tensor_copy(
-                group_cols(first, width).rearrange("p (q r) -> p q r", r=PACK),
-                y[c][:, :, part].rearrange("p r q -> p q r"),
+                group_cols(first, width).rearrange("p (g i r) -> p g r i", i=4, r=PACK),
+                y[c][:, :, part].rearrange("p r (g i) -> p g r i", i=4),
             )
 
         def store(c):

@@ -1,6 +1,7 @@
 from contextlib import ExitStack
 
 import concourse.mybir as mybir
+from concourse.masks import make_identity
 
 N, T, D, NQ = 512, 2048, 512, 512
 FLOPS = 2 * N * D * NQ
@@ -26,22 +27,20 @@ def tile_attend_plw_cap_topk_kernel(tc, qT, k_words, k_scales, ls, offs, out_0, 
     nc = tc.nc
     with ExitStack() as ctx:
         sb = ctx.enter_context(tc.tile_pool(name="sb", bufs=1))
-        late = ctx.enter_context(tc.tile_pool(name="late", bufs=1))
+        shared = ctx.enter_context(tc.tile_pool(name="shared", bufs=1))
         ps = ctx.enter_context(tc.psum_pool(name="ps", bufs=1))
 
-        ls_cols = sb.tile([P, PACK], F32, name="ls_cols")
+        ls_cols = shared.tile([P, PACK], F32, name="ls_cols", offset=4 * T, align_bytes=64)
         nc.scalar.dma_start(ls_cols[:], ls[0, 0, :].rearrange("(n m) -> n m", m=PACK))
 
         q_rows = qT[0].rearrange("(p j) q -> p j q", j=PACK)
-        q_first = sb.tile([P, PACK, QC], F32, name="q_raw0")
-        nc.sync.dma_start(q_first[:], q_rows[:, :, 0:QC])
-        q_raw = [q_first]
+        loads = [(c * QC, QC) for c in range(CHUNKS)]
+        q_raw = [sb.tile([P, PACK, w], F32, name="q_raw%d" % a) for a, w in loads]
+        nc.sync.dma_start(q_raw[0][:], q_rows[:, :, 0:QC])
 
         offsets = sb.tile([P, N // 16], U16, name="offsets")
         nc.sync.dma_start(offsets[:], offs)
 
-        blank = late.tile([P, T + (CHUNKS - 1) * PACK * QC], F32, name="blank", offset=0)
-        nc.vector.memset(blank[:, 0:P], 0.0)
         pool_scales = sb.tile([P, T], U8, name="pool_scales", align_bytes=64)
         nc.vector.memset(pool_scales[:].bitcast(I32), 0)
         for quad in range(4):
@@ -51,72 +50,87 @@ def tile_attend_plw_cap_topk_kernel(tc, qT, k_words, k_scales, ls, offs, out_0, 
                 k_scales[0, 4 * quad : 4 * quad + 4, :].bitcast(I32),
             )
 
-        identity = sb.tile([P, P], F32, name="identity")
-        nc.gpsimd.affine_select(
-            out=identity[:],
-            in_=blank[:, 0:P],
-            pattern=[[-1, P]],
-            compare_op=ALU.not_equal,
-            fill=1.0,
-            base=0,
-            channel_multiplier=1,
-        )
-
-        pool_words = late.tile([P, T], U32, name="pool_words", offset=0)
+        pool_words = shared.tile([P, T], U32, name="pool_words", offset=0, align_bytes=64)
         nc.sync.dma_start(
             pool_words[:].bitcast(I32),
             k_words[0].rearrange("p t r -> p (t r)").bitcast(I32),
         )
+        for i in range(1, CHUNKS):
+            a, w = loads[i]
+            nc.sync.dma_start(q_raw[i][:], q_rows[:, :, a : a + w])
 
-        for c in range(1, CHUNKS):
-            raw = late.tile([P, PACK, QC], F32, name="q_raw%d" % c, offset=4 * (T + (c - 1) * PACK * QC))
-            nc.sync.dma_start(raw[:], q_rows[:, :, c * QC : (c + 1) * QC])
-            q_raw.append(raw)
+        identity = sb.tile([P, P], F32, name="identity")
+        make_identity(nc, identity[:])
+
+        grouped0 = sb.tile([P, QC, PACK], BF16, name="q_grouped0", align_bytes=64)
+        nc.vector.tensor_copy(
+            grouped0[:].rearrange("p (g i) j -> p g j i", i=4),
+            q_raw[0][:].rearrange("p j (g i) -> p g j i", i=4),
+        )
 
         listed_scales = sb.tile([P, N], U8, name="listed_scales", align_bytes=64)
         nc.vector.tensor_copy(listed_scales[:], pool_scales[:].indirect(offsets[:]))
+
+        ls_bank = ps.tile([P, NQ], F32, name="ls_bank")
+        ls_slots = ls_bank[:].rearrange("p (n m) -> p m n", m=PACK)
+        for m in range(PACK):
+            nc.tensor.transpose(ls_slots[:, m, :], ls_cols[:, m : m + 1].to_broadcast([P, P]), identity[:])
+
+        q_words, q_scales = {}, {}
+
+        def quantise_queries(i, grouped):
+            a, w = loads[i]
+            if i == 0:
+                words = sb.tile([P, w], U32, name="q_words%d" % i, align_bytes=64)
+            else:
+                words = shared.tile([P, w], U32, name="q_words%d" % i, offset=4 * a, align_bytes=64)
+            scales = sb.tile([P, w], U8, name="q_scales%d" % i, align_bytes=64)
+            nc.vector.quantize_mx(words[:].bitcast(FP8X4), scales[:], grouped[:].rearrange("p q j -> p (q j)"))
+            for c in range(a // QC, (a + w) // QC):
+                q_words[c] = words[:, c * QC - a : (c + 1) * QC - a]
+                q_scales[c] = scales[:, c * QC - a : (c + 1) * QC - a]
+
+        quantise_queries(0, grouped0)
         key_scales = sb.tile([P, N], U8, name="key_scales", align_bytes=64)
         nc.vector.tensor_copy(
             key_scales[:].rearrange("p (r s) -> p r s", r=PACK),
             listed_scales[:].rearrange("p (s r) -> p r s", r=PACK),
         )
-        key_words = sb.tile([P, N], U32, name="key_words", align_bytes=64)
+
+        key_words = shared.tile([P, N], U32, name="key_words", offset=4 * T, align_bytes=64)
         nc.vector.tensor_copy(
             key_words[:].rearrange("p (r s) -> p s r", r=PACK),
             pool_words[:].indirect(offsets[:]),
         )
 
-        ls_bank = ps.tile([P, PACK, P], F32, name="ls_bank")
-        for m in range(PACK):
-            nc.tensor.transpose(ls_bank[:, m, :], ls_cols[:, m : m + 1].to_broadcast([P, P]), identity[:])
-        ls_rows = sb.tile([P, NQ], F32, name="ls_rows")
-        nc.scalar.copy(ls_rows[:].rearrange("p (n m) -> p n m", m=PACK), ls_bank[:].rearrange("p m n -> p n m"))
+        for c in (1, 2):
+            grouped = sb.tile([P, QC, PACK], BF16, name="q_grouped%d" % c, align_bytes=64)
+            nc.scalar.copy(grouped[:], q_raw[c][:].rearrange("p j q -> p q j"))
+            quantise_queries(c, grouped)
+        grouped3 = shared.tile([P, QC, PACK], BF16, name="q_grouped3", offset=4096, align_bytes=64)
+        nc.vector.tensor_copy(
+            grouped3[:].rearrange("p (g i) j -> p g j i", i=4),
+            q_raw[3][:].rearrange("p j (g i) -> p g j i", i=4),
+        )
+        quantise_queries(3, grouped3)
 
-        scores = []
+        HALF = PACK // 2
+        scores = {}
         for c in range(CHUNKS):
-            grouped = sb.tile([P, QC, PACK], BF16, name="q_grouped%d" % c, tag="slot%d" % c, align_bytes=64)
-            if c < 2:
-                nc.scalar.copy(grouped[:], q_raw[c][:].rearrange("p j q -> p q j"))
-            else:
-                nc.vector.tensor_copy(
-                    grouped[:].rearrange("p (g i) j -> p g j i", i=4),
-                    q_raw[c][:].rearrange("p j (g i) -> p g j i", i=4),
-                )
-            q_words = sb.tile([P, QC], U32, name="q_words%d" % c, align_bytes=64)
-            q_scales = sb.tile([P, QC], U8, name="q_scales%d" % c, align_bytes=64)
-            nc.vector.quantize_mx(q_words[:].bitcast(FP8X4), q_scales[:], grouped[:].rearrange("p q j -> p (q j)"))
-            bank = ps.tile([P, PACK, QC], F32, name="scores%d" % c)
-            for r in range(PACK):
-                nc.tensor.matmul_mx(
-                    out=bank[:, r, :],
-                    lhsT=key_words[:, r * P : (r + 1) * P].bitcast(FP8X4),
-                    lhsT_scale=key_scales[:, r * P : (r + 1) * P],
-                    rhs=q_words[:].bitcast(FP8X4),
-                    rhs_scale=q_scales[:],
-                    start=True,
-                    stop=True,
-                )
-            scores.append(bank)
+            places = HALF if c < 2 else PACK
+            for r0 in range(0, PACK, places):
+                bank = ps.tile([P, places, QC], F32, name="scores%d_%d" % (c, r0))
+                for r in range(r0, r0 + places):
+                    nc.tensor.matmul_mx(
+                        out=bank[:, r - r0, :],
+                        lhsT=key_words[:, r * P : (r + 1) * P].bitcast(FP8X4),
+                        lhsT_scale=key_scales[:, r * P : (r + 1) * P],
+                        rhs=q_words[c].bitcast(FP8X4),
+                        rhs_scale=q_scales[c],
+                        start=True,
+                        stop=True,
+                    )
+                scores[c, r0] = bank
 
         y_words = sb.tile([P, NQ], U32, name="y_words", align_bytes=64)
         y_scales = sb.tile([P, NQ], U8, name="y_scales", align_bytes=64)
@@ -124,23 +138,23 @@ def tile_attend_plw_cap_topk_kernel(tc, qT, k_words, k_scales, ls, offs, out_0, 
         words_out = out_1[0].rearrange("p q u -> p (q u)").bitcast(I32)
         y_grouped = sb.tile([P, NQ * PACK], BF16, name="y_grouped", align_bytes=64)
         y = [sb.tile([P, PACK, QC], F32, name="y%d" % c) for c in range(CHUNKS)]
+        capped = {}
         logits = {}
 
-        def cap(first, width):
-            c, part = first // QC, slice(first % QC, first % QC + width)
-            capped = sb.tile([P, PACK, width], F32, name="capped%d" % first)
-            nc.scalar.activation(capped[:], scores[c][:, :, part], ACT.Tanh, scale=1.0 / CAP)
-            if first == 0:
-                logits[first] = late.tile([P, PACK, width], F32, name="logit0", offset=4 * (T + 2 * PACK * QC))
-            else:
-                logits[first] = sb.tile(
-                    [P, PACK, width], F32, name="logit%d" % first, tag="slot%d" % (len(logits) + 2), align_bytes=64
-                )
+        def cap(c, r0, places, first, width, tag):
+            key = (c, r0, first)
+            capped[key] = sb.tile([P, places, width], F32, name="capped%d_%d_%d" % key, tag=tag)
+            nc.scalar.activation(capped[key][:], scores[c, r0][:, :, first : first + width], ACT.Tanh, scale=1.0 / CAP)
+
+        def shift(c, r0, places, first, width, sources, tag):
+            key = (c, r0, first)
+            logits[key] = sb.tile([P, places, width], F32, name="logit%d_%d_%d" % key, tag=tag)
+            cols = slice(c * QC + first, c * QC + first + width)
             nc.vector.scalar_tensor_tensor(
-                logits[first][:],
-                capped[:],
+                logits[key][:],
+                sources,
                 CAP,
-                ls_rows[:, first : first + width].unsqueeze(1).to_broadcast([P, PACK, width]),
+                ls_bank[:, cols].unsqueeze(1).to_broadcast([P, places, width]),
                 ALU.mult,
                 ALU.subtract,
             )
@@ -148,9 +162,8 @@ def tile_attend_plw_cap_topk_kernel(tc, qT, k_words, k_scales, ls, offs, out_0, 
         def group_cols(first, width):
             return y_grouped[:, first * PACK : (first + width) * PACK]
 
-        def weigh(first, width):
-            c, part = first // QC, slice(first % QC, first % QC + width)
-            nc.scalar.activation(y[c][:, :, part], logits[first][:], ACT.Exp)
+        def weigh(c, r0, places, first, width):
+            nc.scalar.activation(y[c][:, r0 : r0 + places, first : first + width], logits[c, r0, first][:], ACT.Exp)
 
         def group(first, width):
             c, part = first // QC, slice(first % QC, first % QC + width)
@@ -171,29 +184,35 @@ def tile_attend_plw_cap_topk_kernel(tc, qT, k_words, k_scales, ls, offs, out_0, 
             nc.sync.dma_start(words_out[:, cols], y_words[:, cols].bitcast(I32))
 
         tail = QC // 2
-        cap(0, QC)
-        cap(QC, QC)
-        cap(2 * QC, QC)
-        weigh(0, QC)
+        for c in range(2):
+            for r0 in (0, HALF):
+                cap(c, r0, HALF, 0, QC, "cap%d%d" % (c, r0))
+                shift(c, r0, HALF, 0, QC, capped[c, r0, 0][:], "log%d%d" % (c, r0))
+        weigh(0, 0, HALF, 0, QC)
+        weigh(0, HALF, HALF, 0, QC)
         store(0)
-        weigh(QC, QC)
-        store(1)
-        cap(3 * QC, tail)
-        cap(3 * QC + tail, tail)
+        cap(2, 0, PACK, 0, QC, "log00")
         group(0, QC)
+        shift(2, 0, PACK, 0, QC, capped[2, 0, 0][:], "log2")
+        weigh(1, 0, HALF, 0, QC)
+        weigh(1, HALF, HALF, 0, QC)
+        store(1)
+        cap(3, 0, PACK, 0, tail, "log10")
+        cap(3, 0, PACK, tail, tail, "log12")
         group(QC, QC)
+        shift(3, 0, PACK, 0, tail, capped[3, 0, 0][:], "log3a")
+        shift(3, 0, PACK, tail, tail, capped[3, 0, tail][:], "log3b")
+        weigh(2, 0, PACK, 0, QC)
+        store(2)
         planes(0, 2 * QC)
         store_words(0, 2 * QC)
-        weigh(2 * QC, QC)
-        store(2)
         group(2 * QC, QC)
-        weigh(3 * QC, tail)
+        weigh(3, 0, PACK, 0, tail)
         group(3 * QC, tail)
-        weigh(3 * QC + tail, tail)
+        weigh(3, 0, PACK, tail, tail)
         store(3)
         group(3 * QC + tail, tail)
-        planes(2 * QC, QC)
-        planes(3 * QC, QC)
+        planes(2 * QC, 2 * QC)
         store_words(2 * QC, 2 * QC)
         for quad in range(4):
             queue = nc.sync if quad == 0 else nc.scalar

@@ -43,12 +43,9 @@ def tile_attend_plw_cap_topk_kernel(tc, qT, k_words, k_scales, ls, offs, out_0, 
 
         pool_scales = sb.tile([P, T], U8, name="pool_scales", align_bytes=64)
         nc.vector.memset(pool_scales[:].bitcast(I32), 0)
-        for quad in range(4):
-            queue = nc.sync if quad % 2 == 0 else nc.scalar
-            queue.dma_start(
-                pool_scales[32 * quad : 32 * quad + 4, :].bitcast(I32),
-                k_scales[0, 4 * quad : 4 * quad + 4, :].bitcast(I32),
-            )
+        for j in range(4):
+            queue = nc.sync if j % 2 == 0 else nc.scalar
+            queue.dma_start(pool_scales[j:P:32, :].bitcast(I32), k_scales[0, j:16:4, :].bitcast(I32))
 
         pool_words = shared.tile([P, T], U32, name="pool_words", offset=0, align_bytes=64)
         nc.sync.dma_start(
@@ -209,14 +206,15 @@ def tile_attend_plw_cap_topk_kernel(tc, qT, k_words, k_scales, ls, offs, out_0, 
         group(2 * QC, QC)
         weigh(3, 0, PACK, 0, tail)
         group(3 * QC, tail)
+        nc.scalar.activation(
+            group_cols(3 * QC + tail, tail).rearrange("p (q r) -> p q r", r=PACK),
+            logits[3, 0, tail][:].rearrange("p r q -> p q r"),
+            ACT.Exp,
+        )
         weigh(3, 0, PACK, tail, tail)
         store(3)
-        group(3 * QC + tail, tail)
         planes(2 * QC, 2 * QC)
         store_words(2 * QC, 2 * QC)
-        for quad in range(4):
-            queue = nc.sync if quad == 0 else nc.scalar
-            queue.dma_start(
-                out_2[0, 4 * quad : 4 * quad + 4, :].bitcast(I32),
-                y_scales[32 * quad : 32 * quad + 4, :].bitcast(I32),
-            )
+        for j in range(4):
+            queue = nc.sync if j == 0 else nc.scalar
+            queue.dma_start(out_2[0, j:16:4, :].bitcast(I32), y_scales[j:P:32, :].bitcast(I32))

@@ -79,6 +79,8 @@ def tile_attend_plw_cap_topk_kernel(tc, qT, k_words, k_scales, ls, offs, out_0, 
             a, w = loads[i]
             if i == 0:
                 words = sb.tile([P, w], U32, name="q_words%d" % i, align_bytes=64)
+            elif i == 3:
+                words = sb.tile([P, w], U32, name="q_words%d" % i, tag="cap02", align_bytes=64)
             else:
                 words = shared.tile([P, w], U32, name="q_words%d" % i, offset=4 * a, align_bytes=64)
             scales = sb.tile([P, w], U8, name="q_scales%d" % i, align_bytes=64)
@@ -100,67 +102,64 @@ def tile_attend_plw_cap_topk_kernel(tc, qT, k_words, k_scales, ls, offs, out_0, 
             pool_words[:].indirect(offsets[:]),
         )
 
-        for c in (1, 2):
-            grouped = sb.tile([P, QC, PACK], BF16, name="q_grouped%d" % c, align_bytes=64)
-            nc.scalar.copy(grouped[:], q_raw[c][:].rearrange("p j q -> p q j"))
-            quantise_queries(c, grouped)
-        grouped3 = shared.tile([P, QC, PACK], BF16, name="q_grouped3", offset=4096, align_bytes=64)
+        grouped1 = sb.tile([P, QC, PACK], BF16, name="q_grouped1", align_bytes=64)
+        nc.scalar.copy(grouped1[:], q_raw[1][:].rearrange("p j q -> p q j"))
+        quantise_queries(1, grouped1)
+        grouped2 = shared.tile([P, QC, PACK], BF16, name="q_grouped2", offset=4096, align_bytes=64)
         nc.vector.tensor_copy(
-            grouped3[:].rearrange("p (g i) j -> p g j i", i=4),
-            q_raw[3][:].rearrange("p j (g i) -> p g j i", i=4),
+            grouped2[:].rearrange("p (g i) j -> p g j i", i=4),
+            q_raw[2][:].rearrange("p j (g i) -> p g j i", i=4),
         )
-        quantise_queries(3, grouped3)
+        quantise_queries(2, grouped2)
+        grouped3 = sb.tile([P, QC, PACK], BF16, name="q_grouped3", align_bytes=64)
+        nc.gpsimd.tensor_scalar(grouped3[:], q_raw[3][:].rearrange("p j q -> p q j"), 1.0, 0.0, ALU.mult, ALU.add)
 
         HALF = PACK // 2
-        scores = {}
-        for c in range(CHUNKS):
-            places = HALF if c < 2 else PACK
-            for r0 in range(0, PACK, places):
-                bank = ps.tile([P, places, QC], F32, name="scores%d_%d" % (c, r0))
-                for r in range(r0, r0 + places):
-                    nc.tensor.matmul_mx(
-                        out=bank[:, r - r0, :],
-                        lhsT=key_words[:, r * P : (r + 1) * P].bitcast(FP8X4),
-                        lhsT_scale=key_scales[:, r * P : (r + 1) * P],
-                        rhs=q_words[c].bitcast(FP8X4),
-                        rhs_scale=q_scales[c],
-                        start=True,
-                        stop=True,
-                    )
-                scores[c, r0] = bank
 
-        y_words = sb.tile([P, NQ], U32, name="y_words", align_bytes=64)
+        def multiply(c, r0, places):
+            bank = ps.tile([P, places, QC], F32, name="scores%d_%d" % (c, r0))
+            for r in range(r0, r0 + places):
+                nc.tensor.matmul_mx(
+                    out=bank[:, r - r0, :],
+                    lhsT=key_words[:, r * P : (r + 1) * P].bitcast(FP8X4),
+                    lhsT_scale=key_scales[:, r * P : (r + 1) * P],
+                    rhs=q_words[c].bitcast(FP8X4),
+                    rhs_scale=q_scales[c],
+                    start=True,
+                    stop=True,
+                )
+            return bank
+
         y_scales = sb.tile([P, NQ], U8, name="y_scales", align_bytes=64)
         y_rows = out_0.rearrange("(p r) q -> p r q", r=PACK)
         words_out = out_1[0].rearrange("p q u -> p (q u)").bitcast(I32)
         y_grouped = sb.tile([P, NQ * PACK], BF16, name="y_grouped", align_bytes=64)
         y = [sb.tile([P, PACK, QC], F32, name="y%d" % c) for c in range(CHUNKS)]
-        capped = {}
-        logits = {}
 
-        def cap(c, r0, places, first, width, tag):
-            key = (c, r0, first)
-            capped[key] = sb.tile([P, places, width], F32, name="capped%d_%d_%d" % key, tag=tag)
-            nc.scalar.activation(capped[key][:], scores[c, r0][:, :, first : first + width], ACT.Tanh, scale=1.0 / CAP)
+        def staging(shape, name, tag):
+            return sb.tile(shape, F32, name=name, tag=tag, align_bytes=64)
 
-        def shift(c, r0, places, first, width, sources, tag):
-            key = (c, r0, first)
-            logits[key] = sb.tile([P, places, width], F32, name="logit%d_%d_%d" % key, tag=tag)
-            cols = slice(c * QC + first, c * QC + first + width)
+        def cap(out, in_):
+            nc.scalar.activation(out, in_, ACT.Tanh, scale=1.0 / CAP)
+
+        def shift(capped, first, name):
+            places, width = capped.shape[1], capped.shape[2]
+            logit = staging([P, places, width], name, name)
             nc.vector.scalar_tensor_tensor(
-                logits[key][:],
-                sources,
+                logit[:],
+                capped,
                 CAP,
-                ls_bank[:, cols].unsqueeze(1).to_broadcast([P, places, width]),
+                ls_bank[:, first : first + width].unsqueeze(1).to_broadcast([P, places, width]),
                 ALU.mult,
                 ALU.subtract,
             )
+            return logit
 
         def group_cols(first, width):
             return y_grouped[:, first * PACK : (first + width) * PACK]
 
-        def weigh(c, r0, places, first, width):
-            nc.scalar.activation(y[c][:, r0 : r0 + places, first : first + width], logits[c, r0, first][:], ACT.Exp)
+        def weigh(out, logit):
+            nc.scalar.activation(out, logit, ACT.Exp)
 
         def group(first, width):
             c, part = first // QC, slice(first % QC, first % QC + width)
@@ -180,40 +179,50 @@ def tile_attend_plw_cap_topk_kernel(tc, qT, k_words, k_scales, ls, offs, out_0, 
             cols = slice(first, first + width)
             nc.sync.dma_start(words_out[:, cols], y_words[:, cols].bitcast(I32))
 
+        halves = [(c, r0) for c in range(2) for r0 in (0, HALF)]
+        banks = {key: multiply(key[0], key[1], HALF) for key in halves}
+        bank2 = multiply(2, 0, PACK)
+        logits = {}
+        for c, r0 in halves:
+            capped = staging([P, HALF, QC], "capped%d%d" % (c, r0), "cap%d%d" % (c, r0))
+            cap(capped[:], banks[c, r0][:])
+            logits[c, r0] = shift(capped[:], c * QC, "log%d%d" % (c, r0))
+            if (c, r0) == (1, 0):
+                quantise_queries(3, grouped3)
+        bank3 = multiply(3, 0, PACK)
         tail = QC // 2
-        for c in range(2):
-            for r0 in (0, HALF):
-                cap(c, r0, HALF, 0, QC, "cap%d%d" % (c, r0))
-                shift(c, r0, HALF, 0, QC, capped[c, r0, 0][:], "log%d%d" % (c, r0))
-        weigh(0, 0, HALF, 0, QC)
-        weigh(0, HALF, HALF, 0, QC)
+        for r0 in (0, HALF):
+            weigh(y[0][:, r0 : r0 + HALF, :], logits[0, r0][:])
         store(0)
-        cap(2, 0, PACK, 0, QC, "log00")
+        capped2 = staging([P, PACK, QC], "capped2", "log00")
+        cap(capped2[:], bank2[:])
         group(0, QC)
-        shift(2, 0, PACK, 0, QC, capped[2, 0, 0][:], "log2")
-        weigh(1, 0, HALF, 0, QC)
-        weigh(1, HALF, HALF, 0, QC)
+        logits[2] = shift(capped2[:], 2 * QC, "log2")
+        for r0 in (0, HALF):
+            weigh(y[1][:, r0 : r0 + HALF, :], logits[1, r0][:])
         store(1)
-        cap(3, 0, PACK, 0, tail, "log10")
-        cap(3, 0, PACK, tail, tail, "log12")
+        capped3 = staging([P, PACK, QC], "capped3", "log10")
+        for first in (0, tail):
+            cap(capped3[:, :, first : first + tail], bank3[:, :, first : first + tail])
         group(QC, QC)
-        shift(3, 0, PACK, 0, tail, capped[3, 0, 0][:], "log3a")
-        shift(3, 0, PACK, tail, tail, capped[3, 0, tail][:], "log3b")
-        weigh(2, 0, PACK, 0, QC)
+        for first in (0, tail):
+            logits[3, first] = shift(capped3[:, :, first : first + tail], 3 * QC + first, "log3_%d" % first)
+        weigh(y[2][:], logits[2][:])
         store(2)
+        y_words = sb.tile([P, NQ], U32, name="y_words", align_bytes=64)
         planes(0, 2 * QC)
         store_words(0, 2 * QC)
         group(2 * QC, QC)
-        weigh(3, 0, PACK, 0, tail)
+        weigh(y[3][:, :, 0:tail], logits[3, 0][:])
         group(3 * QC, tail)
-        nc.scalar.activation(
+        weigh(
             group_cols(3 * QC + tail, tail).rearrange("p (q r) -> p q r", r=PACK),
-            logits[3, 0, tail][:].rearrange("p r q -> p q r"),
-            ACT.Exp,
+            logits[3, tail][:].rearrange("p r q -> p q r"),
         )
-        weigh(3, 0, PACK, tail, tail)
+        weigh(y[3][:, :, tail:QC], logits[3, tail][:])
         store(3)
-        planes(2 * QC, 2 * QC)
+        planes(2 * QC, QC)
+        planes(3 * QC, QC)
         store_words(2 * QC, 2 * QC)
         for j in range(4):
             queue = nc.sync if j == 0 else nc.scalar

@@ -168,8 +168,9 @@ def tile_attend_plw_cap_topk_kernel(tc, qT, k_words, k_scales, ls, offs, out_0, 
                 y[c][:, :, part].rearrange("p r (g i) -> p g r i", i=4),
             )
 
-        def store(c):
-            nc.sync.dma_start(y_rows[:, :, c * QC : (c + 1) * QC], y[c][:])
+        def store(c, r0=0, places=PACK):
+            rows = slice(r0, r0 + places)
+            nc.sync.dma_start(y_rows[:, rows, c * QC : (c + 1) * QC], y[c][:, rows, :])
 
         def planes(first, width):
             cols = slice(first, first + width)
@@ -200,15 +201,23 @@ def tile_attend_plw_cap_topk_kernel(tc, qT, k_words, k_scales, ls, offs, out_0, 
         logits[2] = shift(capped2[:], 2 * QC, "log2")
         for r0 in (0, HALF):
             weigh(y[1][:, r0 : r0 + HALF, :], logits[1, r0][:])
-        store(1)
+            store(1, r0, HALF)
         capped3 = staging([P, PACK, QC], "capped3", "log10")
         for first in (0, tail):
             cap(capped3[:, :, first : first + tail], bank3[:, :, first : first + tail])
-        group(QC, QC)
+        nc.gpsimd.tensor_scalar(
+            group_cols(QC, QC).rearrange("p (q r) -> p q r", r=PACK),
+            y[1][:].rearrange("p r q -> p q r"),
+            1.0,
+            0.0,
+            ALU.mult,
+            ALU.add,
+        )
         for first in (0, tail):
             logits[3, first] = shift(capped3[:, :, first : first + tail], 3 * QC + first, "log3_%d" % first)
-        weigh(y[2][:], logits[2][:])
-        store(2)
+        for r0 in (0, HALF):
+            weigh(y[2][:, r0 : r0 + HALF, :], logits[2][:, r0 : r0 + HALF, :])
+            store(2, r0, HALF)
         y_words = sb.tile([P, NQ], U32, name="y_words", align_bytes=64)
         planes(0, 2 * QC)
         store_words(0, 2 * QC)
@@ -225,5 +234,4 @@ def tile_attend_plw_cap_topk_kernel(tc, qT, k_words, k_scales, ls, offs, out_0, 
         planes(3 * QC, QC)
         store_words(2 * QC, 2 * QC)
         for j in range(4):
-            queue = nc.sync if j == 0 else nc.scalar
-            queue.dma_start(out_2[0, j:16:4, :].bitcast(I32), y_scales[j:P:32, :].bitcast(I32))
+            nc.scalar.dma_start(out_2[0, j:16:4, :].bitcast(I32), y_scales[j:P:32, :].bitcast(I32))

@@ -43,9 +43,7 @@ def tile_attend_plw_cap_topk_kernel(tc, qT, k_words, k_scales, ls, offs, out_0, 
 
         pool_scales = sb.tile([P, T], U8, name="pool_scales", align_bytes=64)
         nc.vector.memset(pool_scales[:].bitcast(I32), 0)
-        for j in range(4):
-            queue = nc.sync if j % 2 == 0 else nc.scalar
-            queue.dma_start(pool_scales[j:P:32, :].bitcast(I32), k_scales[0, j:16:4, :].bitcast(I32))
+        nc.sync.dma_start(pool_scales[0:P:8, :].bitcast(I32), k_scales[0].bitcast(I32))
 
         pool_words = shared.tile([P, T], U32, name="pool_words", offset=0, align_bytes=64)
         nc.sync.dma_start(
@@ -60,10 +58,7 @@ def tile_attend_plw_cap_topk_kernel(tc, qT, k_words, k_scales, ls, offs, out_0, 
         make_identity(nc, identity[:])
 
         grouped0 = sb.tile([P, QC, PACK], BF16, name="q_grouped0", align_bytes=64)
-        nc.vector.tensor_copy(
-            grouped0[:].rearrange("p (g i) j -> p g j i", i=4),
-            q_raw[0][:].rearrange("p j (g i) -> p g j i", i=4),
-        )
+        nc.scalar.copy(grouped0[:], q_raw[0][:].rearrange("p j q -> p q j"))
 
         listed_scales = sb.tile([P, N], U8, name="listed_scales", align_bytes=64)
         nc.vector.tensor_copy(listed_scales[:], pool_scales[:].indirect(offsets[:]))
@@ -95,6 +90,8 @@ def tile_attend_plw_cap_topk_kernel(tc, qT, k_words, k_scales, ls, offs, out_0, 
             key_scales[:].rearrange("p (r s) -> p r s", r=PACK),
             listed_scales[:].rearrange("p (s r) -> p r s", r=PACK),
         )
+        for j in range(1, 4):
+            nc.scalar.dma_start(key_scales[j:P:32, :].bitcast(I32), key_scales[8 * j : P : 32, :].bitcast(I32))
 
         key_words = shared.tile([P, N], U32, name="key_words", offset=4 * T, align_bytes=64)
         nc.vector.tensor_copy(

@@ -30,35 +30,32 @@ def tile_attend_plw_cap_topk_kernel(tc, qT, k_words, k_scales, ls, offs, out_0, 
         shared = ctx.enter_context(tc.tile_pool(name="shared", bufs=1))
         ps = ctx.enter_context(tc.psum_pool(name="ps", bufs=1))
 
-        ls_cols = shared.tile([P, PACK], F32, name="ls_cols", offset=4 * T, align_bytes=64)
-        nc.scalar.dma_start(ls_cols[:], ls[0, 0, :].rearrange("(n m) -> n m", m=PACK))
-
-        q_rows = qT[0].rearrange("(p j) q -> p j q", j=PACK)
-        loads = [(c * QC, QC) for c in range(CHUNKS)]
-        q_raw = [sb.tile([P, PACK, w], F32, name="q_raw%d" % a) for a, w in loads]
-        nc.sync.dma_start(q_raw[0][:], q_rows[:, :, 0:QC])
+        pool_scales = sb.tile([P, T], U8, name="pool_scales", align_bytes=64)
+        nc.scalar.dma_start(pool_scales[P - 16 : P, :].bitcast(I32), k_scales[0].bitcast(I32))
+        nc.vector.memset(pool_scales[0 : P - 16, :].bitcast(I32), 0)
 
         offsets = sb.tile([P, N // 16], U16, name="offsets")
         nc.sync.dma_start(offsets[:], offs)
 
-        pool_scales = sb.tile([P, T], U8, name="pool_scales", align_bytes=64)
-        nc.vector.memset(pool_scales[:].bitcast(I32), 0)
-        nc.sync.dma_start(pool_scales[0:P:8, :].bitcast(I32), k_scales[0].bitcast(I32))
+        ls_cols = sb.tile([P, PACK], F32, name="ls_cols")
+        nc.sync.dma_start(ls_cols[:], ls[0, 0, :].rearrange("(n m) -> n m", m=PACK))
+        minus_ls = shared.tile([P, PACK], F32, name="minus_ls", offset=4 * T, align_bytes=64)
+        nc.scalar.activation(minus_ls[:], ls_cols[:], ACT.Copy, scale=-1.0)
 
         pool_words = shared.tile([P, T], U32, name="pool_words", offset=0, align_bytes=64)
         nc.sync.dma_start(
             pool_words[:].bitcast(I32),
             k_words[0].rearrange("p t r -> p (t r)").bitcast(I32),
         )
-        for i in range(1, CHUNKS):
+        q_rows = qT[0].rearrange("(p j) q -> p j q", j=PACK)
+        loads = [(c * QC, QC) for c in range(CHUNKS)]
+        q_raw = [sb.tile([P, PACK, w], F32, name="q_raw%d" % a) for a, w in loads]
+        for i in range(CHUNKS):
             a, w = loads[i]
             nc.sync.dma_start(q_raw[i][:], q_rows[:, :, a : a + w])
 
         identity = sb.tile([P, P], F32, name="identity")
         make_identity(nc, identity[:])
-
-        grouped0 = sb.tile([P, QC, PACK], BF16, name="q_grouped0", align_bytes=64)
-        nc.scalar.copy(grouped0[:], q_raw[0][:].rearrange("p j q -> p q j"))
 
         listed_scales = sb.tile([P, N], U8, name="listed_scales", align_bytes=64)
         nc.vector.tensor_copy(listed_scales[:], pool_scales[:].indirect(offsets[:]))
@@ -66,15 +63,13 @@ def tile_attend_plw_cap_topk_kernel(tc, qT, k_words, k_scales, ls, offs, out_0, 
         ls_bank = ps.tile([P, NQ], F32, name="ls_bank")
         ls_slots = ls_bank[:].rearrange("p (n m) -> p m n", m=PACK)
         for m in range(PACK):
-            nc.tensor.transpose(ls_slots[:, m, :], ls_cols[:, m : m + 1].to_broadcast([P, P]), identity[:])
+            nc.tensor.transpose(ls_slots[:, m, :], minus_ls[:, m : m + 1].to_broadcast([P, P]), identity[:])
 
         q_words, q_scales = {}, {}
 
         def quantise_queries(i, grouped):
             a, w = loads[i]
-            if i == 0:
-                words = sb.tile([P, w], U32, name="q_words%d" % i, align_bytes=64)
-            elif i == 3:
+            if i == 3:
                 words = sb.tile([P, w], U32, name="q_words%d" % i, tag="cap02", align_bytes=64)
             else:
                 words = shared.tile([P, w], U32, name="q_words%d" % i, offset=4 * a, align_bytes=64)
@@ -84,14 +79,13 @@ def tile_attend_plw_cap_topk_kernel(tc, qT, k_words, k_scales, ls, offs, out_0, 
                 q_words[c] = words[:, c * QC - a : (c + 1) * QC - a]
                 q_scales[c] = scales[:, c * QC - a : (c + 1) * QC - a]
 
-        quantise_queries(0, grouped0)
         key_scales = sb.tile([P, N], U8, name="key_scales", align_bytes=64)
         nc.vector.tensor_copy(
             key_scales[:].rearrange("p (r s) -> p r s", r=PACK),
             listed_scales[:].rearrange("p (s r) -> p r s", r=PACK),
         )
-        for j in range(1, 4):
-            nc.scalar.dma_start(key_scales[j:P:32, :].bitcast(I32), key_scales[8 * j : P : 32, :].bitcast(I32))
+        for j in range(4):
+            nc.scalar.dma_start(key_scales[j:P:32, :].bitcast(I32), key_scales[P - 16 + j : P : 4, :].bitcast(I32))
 
         key_words = shared.tile([P, N], U32, name="key_words", offset=4 * T, align_bytes=64)
         nc.vector.tensor_copy(
@@ -99,9 +93,10 @@ def tile_attend_plw_cap_topk_kernel(tc, qT, k_words, k_scales, ls, offs, out_0, 
             pool_words[:].indirect(offsets[:]),
         )
 
-        grouped1 = sb.tile([P, QC, PACK], BF16, name="q_grouped1", align_bytes=64)
-        nc.scalar.copy(grouped1[:], q_raw[1][:].rearrange("p j q -> p q j"))
-        quantise_queries(1, grouped1)
+        for c in range(2):
+            grouped = sb.tile([P, QC, PACK], BF16, name="q_grouped%d" % c, align_bytes=64)
+            nc.scalar.copy(grouped[:], q_raw[c][:].rearrange("p j q -> p q j"))
+            quantise_queries(c, grouped)
         grouped2 = shared.tile([P, QC, PACK], BF16, name="q_grouped2", offset=4096, align_bytes=64)
         nc.vector.tensor_copy(
             grouped2[:].rearrange("p (g i) j -> p g j i", i=4),
@@ -148,7 +143,7 @@ def tile_attend_plw_cap_topk_kernel(tc, qT, k_words, k_scales, ls, offs, out_0, 
                 CAP,
                 ls_bank[:, first : first + width].unsqueeze(1).to_broadcast([P, places, width]),
                 ALU.mult,
-                ALU.subtract,
+                ALU.add,
             )
             return logit
 

@@ -49,15 +49,21 @@ def tile_attend_plw_cap_topk_kernel(tc, qT, k_words, k_scales, ls, offs, out_0, 
         )
         q_rows = qT[0].rearrange("(p j) q -> p j q", j=PACK)
         loads = [(c * QC, QC) for c in range(CHUNKS)]
-        q_raw = [sb.tile([P, PACK, w], F32, name="q_raw%d" % a) for a, w in loads]
-        for i in range(CHUNKS):
+        q_raw = {}
+
+        def load_queries(i, tile):
             a, w = loads[i]
-            nc.sync.dma_start(q_raw[i][:], q_rows[:, :, a : a + w])
+            q_raw[i] = tile
+            nc.sync.dma_start(tile[:], q_rows[:, :, a : a + w])
+
+        for i in range(2):
+            load_queries(i, sb.tile([P, PACK, QC], F32, name="q_raw%d" % i))
 
         identity = sb.tile([P, P], F32, name="identity")
         make_identity(nc, identity[:])
 
-        listed_scales = sb.tile([P, N], U8, name="listed_scales", align_bytes=64)
+        late = 4 * T + 4 * N
+        listed_scales = shared.tile([P, N], U8, name="listed_scales", offset=late + 2048 - 256, align_bytes=64)
         nc.vector.tensor_copy(listed_scales[:], pool_scales[:].indirect(offsets[:]))
 
         ls_bank = ps.tile([P, NQ], F32, name="ls_bank")
@@ -85,7 +91,12 @@ def tile_attend_plw_cap_topk_kernel(tc, qT, k_words, k_scales, ls, offs, out_0, 
             listed_scales[:].rearrange("p (s r) -> p r s", r=PACK),
         )
         for j in range(4):
-            nc.scalar.dma_start(key_scales[j:P:32, :].bitcast(I32), key_scales[P - 16 + j : P : 4, :].bitcast(I32))
+            queue = nc.sync if j % 2 else nc.scalar
+            queue.dma_start(key_scales[j:P:32, :].bitcast(I32), key_scales[P - 16 + j : P : 4, :].bitcast(I32))
+        for i in range(2, CHUNKS):
+            load_queries(
+                i, shared.tile([P, PACK, QC], F32, name="q_raw%d" % i, offset=late + 2048 * (i - 2), align_bytes=64)
+            )
 
         key_words = shared.tile([P, N], U32, name="key_words", offset=4 * T, align_bytes=64)
         nc.vector.tensor_copy(

@@ -106,7 +106,10 @@ def tile_attend_plw_cap_topk_kernel(tc, qT, k_words, k_scales, ls, offs, out_0, 
 
         for c in range(2):
             grouped = sb.tile([P, QC, PACK], BF16, name="q_grouped%d" % c, align_bytes=64)
-            nc.scalar.copy(grouped[:], q_raw[c][:].rearrange("p j q -> p q j"))
+            nc.scalar.copy(
+                grouped[:].rearrange("p (g i) j -> p g j i", i=4),
+                q_raw[c][:].rearrange("p j (g i) -> p g j i", i=4),
+            )
             quantise_queries(c, grouped)
         grouped2 = shared.tile([P, QC, PACK], BF16, name="q_grouped2", offset=4096, align_bytes=64)
         nc.vector.tensor_copy(
@@ -184,12 +187,17 @@ def tile_attend_plw_cap_topk_kernel(tc, qT, k_words, k_scales, ls, offs, out_0, 
             nc.sync.dma_start(words_out[:, cols], y_words[:, cols].bitcast(I32))
 
         halves = [(c, r0) for c in range(2) for r0 in (0, HALF)]
-        banks = {key: multiply(key[0], key[1], HALF) for key in halves}
+        opening = [multiply(0, r, 1) for r in range(HALF)]
+        banks = {key: multiply(key[0], key[1], HALF) for key in halves[1:]}
         bank2 = multiply(2, 0, PACK)
         logits = {}
         for c, r0 in halves:
             capped = staging([P, HALF, QC], "capped%d%d" % (c, r0), "cap%d%d" % (c, r0))
-            cap(capped[:], banks[c, r0][:])
+            if (c, r0) == (0, 0):
+                for r in range(HALF):
+                    cap(capped[:, r : r + 1, :], opening[r][:])
+            else:
+                cap(capped[:], banks[c, r0][:])
             logits[c, r0] = shift(capped[:], c * QC, "log%d%d" % (c, r0))
             if (c, r0) == (1, 0):
                 quantise_queries(3, grouped3)

@@ -64,7 +64,11 @@ def tile_attend_plw_cap_topk_kernel(tc, qT, k_words, k_scales, ls, offs, out_0, 
 
         late = 4 * T + 4 * N
         listed_scales = shared.tile([P, N], U8, name="listed_scales", offset=late + 2048 - 256, align_bytes=64)
-        nc.vector.tensor_copy(listed_scales[:], pool_scales[:].indirect(offsets[:]))
+        for h in range(2):
+            nc.vector.tensor_copy(
+                listed_scales[:, h * N // 2 : (h + 1) * N // 2],
+                pool_scales[:].indirect(offsets[:, h * N // 32 : (h + 1) * N // 32]),
+            )
 
         ls_bank = ps.tile([P, NQ], F32, name="ls_bank")
         ls_slots = ls_bank[:].rearrange("p (n m) -> p m n", m=PACK)
@@ -86,10 +90,11 @@ def tile_attend_plw_cap_topk_kernel(tc, qT, k_words, k_scales, ls, offs, out_0, 
                 q_scales[c] = scales[:, c * QC - a : (c + 1) * QC - a]
 
         key_scales = sb.tile([P, N], U8, name="key_scales", align_bytes=64)
-        nc.vector.tensor_copy(
-            key_scales[:].rearrange("p (r s) -> p r s", r=PACK),
-            listed_scales[:].rearrange("p (s r) -> p r s", r=PACK),
-        )
+        for h in range(2):
+            nc.vector.tensor_copy(
+                key_scales[:].rearrange("p (r s) -> p r s", r=PACK)[:, :, h * P // 2 : (h + 1) * P // 2],
+                listed_scales[:, h * N // 2 : (h + 1) * N // 2].rearrange("p (s r) -> p r s", r=PACK),
+            )
         for j in range(4):
             queue = nc.sync if j % 2 else nc.scalar
             queue.dma_start(key_scales[j:P:32, :].bitcast(I32), key_scales[P - 16 + j : P : 4, :].bitcast(I32))
@@ -214,8 +219,8 @@ def tile_attend_plw_cap_topk_kernel(tc, qT, k_words, k_scales, ls, offs, out_0, 
             weigh(y[1][:, r0 : r0 + HALF, :], logits[1, r0][:])
             store(1, r0, HALF)
         capped3 = staging([P, PACK, QC], "capped3", "log10")
-        for first in (0, tail):
-            cap(capped3[:, :, first : first + tail], bank3[:, :, first : first + tail])
+        for r0 in (0, HALF):
+            cap(capped3[:, r0 : r0 + HALF, :], bank3[:, r0 : r0 + HALF, :])
         nc.gpsimd.tensor_scalar(
             group_cols(QC, QC).rearrange("p (q r) -> p q r", r=PACK),
             y[1][:].rearrange("p r q -> p q r"),
@@ -224,8 +229,16 @@ def tile_attend_plw_cap_topk_kernel(tc, qT, k_words, k_scales, ls, offs, out_0, 
             ALU.mult,
             ALU.add,
         )
-        for first in (0, tail):
-            logits[3, first] = shift(capped3[:, :, first : first + tail], 3 * QC + first, "log3_%d" % first)
+        logit3 = staging([P, PACK, QC], "log3", "log3")
+        for r0 in (0, HALF):
+            nc.vector.scalar_tensor_tensor(
+                logit3[:, r0 : r0 + HALF, :],
+                capped3[:, r0 : r0 + HALF, :],
+                CAP,
+                ls_bank[:, 3 * QC : 4 * QC].unsqueeze(1).to_broadcast([P, HALF, QC]),
+                ALU.mult,
+                ALU.add,
+            )
         for r0 in (0, HALF):
             weigh(y[2][:, r0 : r0 + HALF, :], logits[2][:, r0 : r0 + HALF, :])
             store(2, r0, HALF)
@@ -233,16 +246,19 @@ def tile_attend_plw_cap_topk_kernel(tc, qT, k_words, k_scales, ls, offs, out_0, 
         planes(0, 2 * QC)
         store_words(0, 2 * QC)
         group(2 * QC, QC)
-        weigh(y[3][:, :, 0:tail], logits[3, 0][:])
+        weigh(y[3][:, 0:HALF, :], logit3[:, 0:HALF, :])
+        store(3, 0, HALF)
+        weigh(y[3][:, HALF:PACK, 0:tail], logit3[:, HALF:PACK, 0:tail])
         group(3 * QC, tail)
         weigh(
             group_cols(3 * QC + tail, tail).rearrange("p (q r) -> p q r", r=PACK),
-            logits[3, tail][:].rearrange("p r q -> p q r"),
+            logit3[:, :, tail:QC].rearrange("p r q -> p q r"),
         )
-        weigh(y[3][:, :, tail:QC], logits[3, tail][:])
-        store(3)
+        weigh(y[3][:, HALF:PACK, tail:QC], logit3[:, HALF:PACK, tail:QC])
+        store(3, HALF, HALF)
         planes(2 * QC, QC)
         planes(3 * QC, QC)
         store_words(2 * QC, 2 * QC)
         for j in range(4):
-            nc.scalar.dma_start(out_2[0, j:16:4, :].bitcast(I32), y_scales[j:P:32, :].bitcast(I32))
+            queue = nc.sync if j == 3 else nc.scalar
+            queue.dma_start(out_2[0, j:16:4, :].bitcast(I32), y_scales[j:P:32, :].bitcast(I32))

@@ -39,8 +39,9 @@ def tile_attend_plw_cap_topk_kernel(tc, qT, k_words, k_scales, ls, offs, out_0, 
 
         ls_cols = sb.tile([P, PACK], F32, name="ls_cols")
         nc.sync.dma_start(ls_cols[:], ls[0, 0, :].rearrange("(n m) -> n m", m=PACK))
-        minus_ls = shared.tile([P, PACK], F32, name="minus_ls", offset=4 * T, align_bytes=64)
-        nc.scalar.activation(minus_ls[:], ls_cols[:], ACT.Copy, scale=-1.0)
+        early = 4 * T + 4 * N
+        minus_ls = shared.tile([P, 80], F32, name="minus_ls", offset=early - 64, align_bytes=64)
+        nc.scalar.activation(minus_ls[:, 0:PACK], ls_cols[:], ACT.Copy, scale=-1.0 / CAP)
 
         pool_words = shared.tile([P, T], U32, name="pool_words", offset=0, align_bytes=64)
         nc.sync.dma_start(
@@ -62,7 +63,7 @@ def tile_attend_plw_cap_topk_kernel(tc, qT, k_words, k_scales, ls, offs, out_0, 
         identity = sb.tile([P, P], F32, name="identity")
         make_identity(nc, identity[:])
 
-        late = 4 * T + 4 * N
+        late = early + 2 * QC
         listed_scales = shared.tile([P, N], U8, name="listed_scales", offset=late + 2048 - 256, align_bytes=64)
         for h in range(2):
             nc.vector.tensor_copy(
@@ -71,7 +72,7 @@ def tile_attend_plw_cap_topk_kernel(tc, qT, k_words, k_scales, ls, offs, out_0, 
             )
 
         ls_bank = ps.tile([P, NQ], F32, name="ls_bank")
-        ls_slots = ls_bank[:].rearrange("p (n m) -> p m n", m=PACK)
+        ls_slots = ls_bank[:].rearrange("p (m n) -> p m n", m=PACK)
         for m in range(PACK):
             nc.tensor.transpose(ls_slots[:, m, :], minus_ls[:, m : m + 1].to_broadcast([P, P]), identity[:])
 
@@ -82,8 +83,11 @@ def tile_attend_plw_cap_topk_kernel(tc, qT, k_words, k_scales, ls, offs, out_0, 
             if i == 3:
                 words = sb.tile([P, w], U32, name="q_words%d" % i, tag="cap02", align_bytes=64)
             else:
-                words = shared.tile([P, w], U32, name="q_words%d" % i, offset=4 * a, align_bytes=64)
-            scales = sb.tile([P, w], U8, name="q_scales%d" % i, align_bytes=64)
+                words = sb.tile([P, w], U32, name="q_words%d" % i, align_bytes=64)
+            if i < 2:
+                scales = shared.tile([P, w], U8, name="q_scales%d" % i, offset=early + a, align_bytes=64)
+            else:
+                scales = sb.tile([P, w], U8, name="q_scales%d" % i, align_bytes=64)
             nc.vector.quantize_mx(words[:].bitcast(FP8X4), scales[:], grouped[:].rearrange("p q j -> p (q j)"))
             for c in range(a // QC, (a + w) // QC):
                 q_words[c] = words[:, c * QC - a : (c + 1) * QC - a]
@@ -153,24 +157,26 @@ def tile_attend_plw_cap_topk_kernel(tc, qT, k_words, k_scales, ls, offs, out_0, 
         def cap(out, in_):
             nc.scalar.activation(out, in_, ACT.Tanh, scale=1.0 / CAP)
 
-        def shift(capped, first, name):
+        def add_ls(logit, capped, first):
             places, width = capped.shape[1], capped.shape[2]
-            logit = staging([P, places, width], name, name)
-            nc.vector.scalar_tensor_tensor(
-                logit[:],
-                capped,
-                CAP,
-                ls_bank[:, first : first + width].unsqueeze(1).to_broadcast([P, places, width]),
-                ALU.mult,
+            by_query = ls_slots.rearrange("p m n -> p n m")[:, first // PACK : (first + width) // PACK, :]
+            nc.vector.tensor_tensor(
+                logit.rearrange("p r (n m) -> p r n m", m=PACK),
+                capped.rearrange("p r (n m) -> p r n m", m=PACK),
+                by_query.unsqueeze(1).to_broadcast([P, places, width // PACK, PACK]),
                 ALU.add,
             )
+
+        def shift(capped, first, name):
+            logit = staging([P, capped.shape[1], capped.shape[2]], name, name)
+            add_ls(logit[:], capped, first)
             return logit
 
         def group_cols(first, width):
             return y_grouped[:, first * PACK : (first + width) * PACK]
 
         def weigh(out, logit):
-            nc.scalar.activation(out, logit, ACT.Exp)
+            nc.scalar.activation(out, logit, ACT.Exp, scale=CAP)
 
         def group(first, width):
             c, part = first // QC, slice(first % QC, first % QC + width)
@@ -231,14 +237,7 @@ def tile_attend_plw_cap_topk_kernel(tc, qT, k_words, k_scales, ls, offs, out_0, 
         )
         logit3 = staging([P, PACK, QC], "log3", "log3")
         for r0 in (0, HALF):
-            nc.vector.scalar_tensor_tensor(
-                logit3[:, r0 : r0 + HALF, :],
-                capped3[:, r0 : r0 + HALF, :],
-                CAP,
-                ls_bank[:, 3 * QC : 4 * QC].unsqueeze(1).to_broadcast([P, HALF, QC]),
-                ALU.mult,
-                ALU.add,
-            )
+            add_ls(logit3[:, r0 : r0 + HALF, :], capped3[:, r0 : r0 + HALF, :], 3 * QC)
         for r0 in (0, HALF):
             weigh(y[2][:, r0 : r0 + HALF, :], logits[2][:, r0 : r0 + HALF, :])
             store(2, r0, HALF)

@@ -38,9 +38,9 @@ def tile_attend_plw_cap_topk_kernel(tc, qT, k_words, k_scales, ls, offs, out_0, 
         nc.sync.dma_start(offsets[:], offs)
 
         ls_cols = sb.tile([P, PACK], F32, name="ls_cols")
-        nc.sync.dma_start(ls_cols[:], ls[0, 0, :].rearrange("(n m) -> n m", m=PACK))
+        nc.scalar.dma_start(ls_cols[:], ls[0, 0, :].rearrange("(n m) -> n m", m=PACK))
         early = 4 * T + 4 * N
-        minus_ls = shared.tile([P, 80], F32, name="minus_ls", offset=early - 64, align_bytes=64)
+        minus_ls = shared.tile([P, 80], F32, name="minus_ls", offset=early, align_bytes=64)
         nc.scalar.activation(minus_ls[:, 0:PACK], ls_cols[:], ACT.Copy, scale=-1.0 / CAP)
 
         pool_words = shared.tile([P, T], U32, name="pool_words", offset=0, align_bytes=64)
@@ -63,7 +63,7 @@ def tile_attend_plw_cap_topk_kernel(tc, qT, k_words, k_scales, ls, offs, out_0, 
         identity = sb.tile([P, P], F32, name="identity")
         make_identity(nc, identity[:])
 
-        late = early + 2 * QC
+        late = early + 2 * QC + 2 * PACK * QC
         listed_scales = shared.tile([P, N], U8, name="listed_scales", offset=late + 2048 - 256, align_bytes=64)
         for h in range(2):
             nc.vector.tensor_copy(
@@ -82,6 +82,8 @@ def tile_attend_plw_cap_topk_kernel(tc, qT, k_words, k_scales, ls, offs, out_0, 
             a, w = loads[i]
             if i == 3:
                 words = sb.tile([P, w], U32, name="q_words%d" % i, tag="cap02", align_bytes=64)
+            elif i < 2:
+                words = shared.tile([P, w], U32, name="q_words%d" % i, offset=4 * a, align_bytes=64)
             else:
                 words = sb.tile([P, w], U32, name="q_words%d" % i, align_bytes=64)
             if i < 2:
@@ -100,8 +102,7 @@ def tile_attend_plw_cap_topk_kernel(tc, qT, k_words, k_scales, ls, offs, out_0, 
                 listed_scales[:, h * N // 2 : (h + 1) * N // 2].rearrange("p (s r) -> p r s", r=PACK),
             )
         for j in range(4):
-            queue = nc.sync if j % 2 else nc.scalar
-            queue.dma_start(key_scales[j:P:32, :].bitcast(I32), key_scales[P - 16 + j : P : 4, :].bitcast(I32))
+            nc.sync.dma_start(key_scales[j:P:32, :].bitcast(I32), key_scales[P - 16 + j : P : 4, :].bitcast(I32))
         for i in range(2, CHUNKS):
             load_queries(
                 i, shared.tile([P, PACK, QC], F32, name="q_raw%d" % i, offset=late + 2048 * (i - 2), align_bytes=64)
@@ -120,13 +121,13 @@ def tile_attend_plw_cap_topk_kernel(tc, qT, k_words, k_scales, ls, offs, out_0, 
                 q_raw[c][:].rearrange("p j (g i) -> p g j i", i=4),
             )
             quantise_queries(c, grouped)
-        grouped2 = shared.tile([P, QC, PACK], BF16, name="q_grouped2", offset=4096, align_bytes=64)
+        grouped2 = shared.tile([P, QC, PACK], BF16, name="q_grouped2", offset=early + 2 * QC, align_bytes=64)
         nc.vector.tensor_copy(
             grouped2[:].rearrange("p (g i) j -> p g j i", i=4),
             q_raw[2][:].rearrange("p j (g i) -> p g j i", i=4),
         )
         quantise_queries(2, grouped2)
-        grouped3 = sb.tile([P, QC, PACK], BF16, name="q_grouped3", align_bytes=64)
+        grouped3 = shared.tile([P, QC, PACK], BF16, name="q_grouped3", offset=early + 2 * QC, align_bytes=64)
         nc.gpsimd.tensor_scalar(grouped3[:], q_raw[3][:].rearrange("p j q -> p q j"), 1.0, 0.0, ALU.mult, ALU.add)
 
         HALF = PACK // 2

@@ -127,8 +127,6 @@ def tile_attend_plw_cap_topk_kernel(tc, qT, k_words, k_scales, ls, offs, out_0, 
             q_raw[2][:].rearrange("p j (g i) -> p g j i", i=4),
         )
         quantise_queries(2, grouped2)
-        grouped3 = shared.tile([P, QC, PACK], BF16, name="q_grouped3", offset=early + 2 * QC, align_bytes=64)
-        nc.gpsimd.tensor_scalar(grouped3[:], q_raw[3][:].rearrange("p j q -> p q j"), 1.0, 0.0, ALU.mult, ALU.add)
 
         HALF = PACK // 2
 
@@ -190,13 +188,10 @@ def tile_attend_plw_cap_topk_kernel(tc, qT, k_words, k_scales, ls, offs, out_0, 
             rows = slice(r0, r0 + places)
             nc.sync.dma_start(y_rows[:, rows, c * QC : (c + 1) * QC], y[c][:, rows, :])
 
-        def planes(first, width):
-            cols = slice(first, first + width)
-            nc.vector.quantize_mx(y_words[:, cols].bitcast(FP8X4), y_scales[:, cols], group_cols(first, width))
-
-        def store_words(first, width):
-            cols = slice(first, first + width)
-            nc.sync.dma_start(words_out[:, cols], y_words[:, cols].bitcast(I32))
+        def planes(words, at, first, width):
+            nc.vector.quantize_mx(
+                words[:, at : at + width].bitcast(FP8X4), y_scales[:, first : first + width], group_cols(first, width)
+            )
 
         halves = [(c, r0) for c in range(2) for r0 in (0, HALF)]
         opening = [multiply(0, r, 1) for r in range(HALF)]
@@ -211,6 +206,12 @@ def tile_attend_plw_cap_topk_kernel(tc, qT, k_words, k_scales, ls, offs, out_0, 
             else:
                 cap(capped[:], banks[c, r0][:])
             logits[c, r0] = shift(capped[:], c * QC, "log%d%d" % (c, r0))
+            if (c, r0) == (0, HALF):
+                grouped3 = sb.tile([P, QC, PACK], BF16, name="q_grouped3", tag="cap00", align_bytes=64)
+                nc.vector.tensor_copy(
+                    grouped3[:].rearrange("p (g i) j -> p g j i", i=4),
+                    q_raw[3][:].rearrange("p j (g i) -> p g j i", i=4),
+                )
             if (c, r0) == (1, 0):
                 quantise_queries(3, grouped3)
         bank3 = multiply(3, 0, PACK)
@@ -222,43 +223,36 @@ def tile_attend_plw_cap_topk_kernel(tc, qT, k_words, k_scales, ls, offs, out_0, 
         cap(capped2[:], bank2[:])
         group(0, QC)
         logits[2] = shift(capped2[:], 2 * QC, "log2")
+        first_words = sb.tile([P, 2 * QC], U32, name="first_words", align_bytes=64)
+        planes(first_words, 0, 0, QC)
         for r0 in (0, HALF):
             weigh(y[1][:, r0 : r0 + HALF, :], logits[1, r0][:])
             store(1, r0, HALF)
-        capped3 = staging([P, PACK, QC], "capped3", "log10")
-        for r0 in (0, HALF):
-            cap(capped3[:, r0 : r0 + HALF, :], bank3[:, r0 : r0 + HALF, :])
-        nc.gpsimd.tensor_scalar(
-            group_cols(QC, QC).rearrange("p (q r) -> p q r", r=PACK),
-            y[1][:].rearrange("p r q -> p q r"),
-            1.0,
-            0.0,
-            ALU.mult,
-            ALU.add,
-        )
-        logit3 = staging([P, PACK, QC], "log3", "log3")
-        for r0 in (0, HALF):
-            add_ls(logit3[:, r0 : r0 + HALF, :], capped3[:, r0 : r0 + HALF, :], 3 * QC)
+        parts = [slice(0, tail), slice(tail, QC)]
+        capped3 = [staging([P, PACK, tail], "capped3%d" % h, "log1%d" % (h * HALF)) for h in range(2)]
+        for h in range(2):
+            cap(capped3[h][:], bank3[:, :, parts[h]])
+        group(QC, QC)
+        logit3 = [shift(capped3[h][:], 3 * QC + h * tail, "log3%d" % h) for h in range(2)]
         for r0 in (0, HALF):
             weigh(y[2][:, r0 : r0 + HALF, :], logits[2][:, r0 : r0 + HALF, :])
             store(2, r0, HALF)
-        y_words = sb.tile([P, NQ], U32, name="y_words", align_bytes=64)
-        planes(0, 2 * QC)
-        store_words(0, 2 * QC)
+        planes(first_words, QC, QC, QC)
+        nc.sync.dma_start(words_out[:, 0 : 2 * QC], first_words[:].bitcast(I32))
         group(2 * QC, QC)
-        weigh(y[3][:, 0:HALF, :], logit3[:, 0:HALF, :])
-        store(3, 0, HALF)
-        weigh(y[3][:, HALF:PACK, 0:tail], logit3[:, HALF:PACK, 0:tail])
+        weigh(y[3][:, :, parts[0]], logit3[0][:])
         group(3 * QC, tail)
         weigh(
             group_cols(3 * QC + tail, tail).rearrange("p (q r) -> p q r", r=PACK),
-            logit3[:, :, tail:QC].rearrange("p r q -> p q r"),
+            logit3[1][:].rearrange("p r q -> p q r"),
         )
-        weigh(y[3][:, HALF:PACK, tail:QC], logit3[:, HALF:PACK, tail:QC])
-        store(3, HALF, HALF)
-        planes(2 * QC, QC)
-        planes(3 * QC, QC)
-        store_words(2 * QC, 2 * QC)
+        for r0 in (0, HALF):
+            weigh(y[3][:, r0 : r0 + HALF, parts[1]], logit3[1][:, r0 : r0 + HALF, :])
+            store(3, r0, HALF)
+        later_words = sb.tile([P, 2 * QC], U32, name="later_words", align_bytes=64)
+        planes(later_words, 0, 2 * QC, QC)
+        planes(later_words, QC, 3 * QC, QC)
+        nc.sync.dma_start(words_out[:, 2 * QC : NQ], later_words[:].bitcast(I32))
         for j in range(4):
             queue = nc.sync if j == 3 else nc.scalar
             queue.dma_start(out_2[0, j:16:4, :].bitcast(I32), y_scales[j:P:32, :].bitcast(I32))

@@ -30,45 +30,49 @@ def tile_attend_plw_cap_topk_kernel(tc, qT, k_words, k_scales, ls, offs, out_0, 
         shared = ctx.enter_context(tc.tile_pool(name="shared", bufs=1))
         ps = ctx.enter_context(tc.psum_pool(name="ps", bufs=1))
 
-        pool_scales = sb.tile([P, T], U8, name="pool_scales", align_bytes=64)
+        raw_bytes = 4 * PACK * QC
+        late = 4 * T
+        early = late + 2 * raw_bytes
+        spread_at = early + 2 * QC + N + 4 * QC
+
+        pool_scales = shared.tile([P, T], U8, name="pool_scales", offset=late + raw_bytes // 2, align_bytes=64)
         nc.scalar.dma_start(pool_scales[P - 16 : P, :].bitcast(I32), k_scales[0].bitcast(I32))
         nc.vector.memset(pool_scales[0 : P - 16, :].bitcast(I32), 0)
+        spread = sb.tile([P, N], U8, name="spread", align_bytes=64)
+        nc.vector.memset(spread[:].bitcast(I32), 0)
 
         offsets = sb.tile([P, N // 16], U16, name="offsets")
         nc.sync.dma_start(offsets[:], offs)
-
-        ls_cols = sb.tile([P, PACK], F32, name="ls_cols")
-        nc.scalar.dma_start(ls_cols[:], ls[0, 0, :].rearrange("(n m) -> n m", m=PACK))
-        early = 4 * T + 4 * N
-        minus_ls = shared.tile([P, 80], F32, name="minus_ls", offset=early, align_bytes=64)
-        nc.scalar.activation(minus_ls[:, 0:PACK], ls_cols[:], ACT.Copy, scale=-1.0 / CAP)
-
         pool_words = shared.tile([P, T], U32, name="pool_words", offset=0, align_bytes=64)
         nc.sync.dma_start(
             pool_words[:].bitcast(I32),
             k_words[0].rearrange("p t r -> p (t r)").bitcast(I32),
         )
+        ls_cols = sb.tile([P, PACK], F32, name="ls_cols")
+        nc.sync.dma_start(ls_cols[:], ls[0, 0, :].rearrange("(n m) -> n m", m=PACK))
+        minus_ls = shared.tile([P, 80], F32, name="minus_ls", offset=early, align_bytes=64)
+        nc.scalar.activation(minus_ls[:, 0:PACK], ls_cols[:], ACT.Copy, scale=-1.0 / CAP)
+
         q_rows = qT[0].rearrange("(p j) q -> p j q", j=PACK)
-        loads = [(c * QC, QC) for c in range(CHUNKS)]
         q_raw = {}
 
-        def load_queries(i, tile):
-            a, w = loads[i]
-            q_raw[i] = tile
-            nc.sync.dma_start(tile[:], q_rows[:, :, a : a + w])
+        def load_queries(c, tile):
+            q_raw[c] = tile
+            nc.sync.dma_start(tile[:], q_rows[:, :, c * QC : (c + 1) * QC])
 
-        for i in range(2):
-            load_queries(i, sb.tile([P, PACK, QC], F32, name="q_raw%d" % i))
+        for c in range(2):
+            load_queries(c, sb.tile([P, PACK, QC], F32, name="q_raw%d" % c))
 
         identity = sb.tile([P, P], F32, name="identity")
         make_identity(nc, identity[:])
 
-        late = early + 2 * QC + 2 * PACK * QC
-        listed_scales = shared.tile([P, N], U8, name="listed_scales", offset=late + 2048 - 256, align_bytes=64)
-        for h in range(2):
-            nc.vector.tensor_copy(
-                listed_scales[:, h * N // 2 : (h + 1) * N // 2],
-                pool_scales[:].indirect(offsets[:, h * N // 32 : (h + 1) * N // 32]),
+        listed_scales = shared.tile([P, N], U8, name="listed_scales", offset=spread_at - N // 2, align_bytes=64)
+        nc.vector.tensor_copy(listed_scales[:], pool_scales[:].indirect(offsets[:]))
+        for j in range(4):
+            nc.sync.dma_start(spread[j:P:32, :].bitcast(I32), listed_scales[P - 16 + j : P : 4, :].bitcast(I32))
+        for c in range(2, CHUNKS):
+            load_queries(
+                c, shared.tile([P, PACK, QC], F32, name="q_raw%d" % c, offset=late + raw_bytes * (c - 2), align_bytes=64)
             )
 
         ls_bank = ps.tile([P, NQ], F32, name="ls_bank")
@@ -76,56 +80,48 @@ def tile_attend_plw_cap_topk_kernel(tc, qT, k_words, k_scales, ls, offs, out_0, 
         for m in range(PACK):
             nc.tensor.transpose(ls_slots[:, m, :], minus_ls[:, m : m + 1].to_broadcast([P, P]), identity[:])
 
-        q_words, q_scales = {}, {}
-
-        def quantise_queries(i, grouped):
-            a, w = loads[i]
-            if i == 3:
-                words = sb.tile([P, w], U32, name="q_words%d" % i, tag="cap02", align_bytes=64)
-            elif i < 2:
-                words = shared.tile([P, w], U32, name="q_words%d" % i, offset=4 * a, align_bytes=64)
-            else:
-                words = sb.tile([P, w], U32, name="q_words%d" % i, align_bytes=64)
-            if i < 2:
-                scales = shared.tile([P, w], U8, name="q_scales%d" % i, offset=early + a, align_bytes=64)
-            else:
-                scales = sb.tile([P, w], U8, name="q_scales%d" % i, align_bytes=64)
-            nc.vector.quantize_mx(words[:].bitcast(FP8X4), scales[:], grouped[:].rearrange("p q j -> p (q j)"))
-            for c in range(a // QC, (a + w) // QC):
-                q_words[c] = words[:, c * QC - a : (c + 1) * QC - a]
-                q_scales[c] = scales[:, c * QC - a : (c + 1) * QC - a]
-
-        key_scales = sb.tile([P, N], U8, name="key_scales", align_bytes=64)
-        for h in range(2):
-            nc.vector.tensor_copy(
-                key_scales[:].rearrange("p (r s) -> p r s", r=PACK)[:, :, h * P // 2 : (h + 1) * P // 2],
-                listed_scales[:, h * N // 2 : (h + 1) * N // 2].rearrange("p (s r) -> p r s", r=PACK),
-            )
-        for j in range(4):
-            nc.sync.dma_start(key_scales[j:P:32, :].bitcast(I32), key_scales[P - 16 + j : P : 4, :].bitcast(I32))
-        for i in range(2, CHUNKS):
-            load_queries(
-                i, shared.tile([P, PACK, QC], F32, name="q_raw%d" % i, offset=late + 2048 * (i - 2), align_bytes=64)
-            )
-
-        key_words = shared.tile([P, N], U32, name="key_words", offset=4 * T, align_bytes=64)
+        key_words = sb.tile([P, N], U32, name="key_words", align_bytes=64)
         nc.vector.tensor_copy(
             key_words[:].rearrange("p (r s) -> p s r", r=PACK),
             pool_words[:].indirect(offsets[:]),
         )
 
-        for c in range(2):
-            grouped = sb.tile([P, QC, PACK], BF16, name="q_grouped%d" % c, align_bytes=64)
-            nc.scalar.copy(
+        q_words, q_scales = {}, {}
+
+        def round_queries(copy, grouped, c):
+            copy(
                 grouped[:].rearrange("p (g i) j -> p g j i", i=4),
                 q_raw[c][:].rearrange("p j (g i) -> p g j i", i=4),
             )
-            quantise_queries(c, grouped)
-        grouped2 = shared.tile([P, QC, PACK], BF16, name="q_grouped2", offset=early + 2 * QC, align_bytes=64)
-        nc.vector.tensor_copy(
-            grouped2[:].rearrange("p (g i) j -> p g j i", i=4),
-            q_raw[2][:].rearrange("p j (g i) -> p g j i", i=4),
-        )
+
+        def quantise_queries(c, grouped):
+            if c == 0:
+                words = shared.tile([P, QC], U32, name="q_words0", offset=0, align_bytes=64)
+            elif c == 1:
+                words = shared.tile([P, QC], U32, name="q_words1", offset=spread_at - 4 * QC, align_bytes=64)
+            else:
+                words = sb.tile([P, QC], U32, name="q_words%d" % c, tag="cap02" if c == 3 else "", align_bytes=64)
+            if c < 2:
+                scales = shared.tile([P, QC], U8, name="q_scales%d" % c, offset=early + c * QC, align_bytes=64)
+            else:
+                scales = sb.tile([P, QC], U8, name="q_scales%d" % c, align_bytes=64)
+            nc.vector.quantize_mx(words[:].bitcast(FP8X4), scales[:], grouped[:].rearrange("p q j -> p (q j)"))
+            q_words[c], q_scales[c] = words[:], scales[:]
+
+        grouped0 = sb.tile([P, QC, PACK], BF16, name="q_grouped0", align_bytes=64)
+        round_queries(nc.scalar.copy, grouped0, 0)
+        quantise_queries(0, grouped0)
+        key_scales = shared.tile([P, N], U8, name="key_scales", offset=early + 2 * QC, align_bytes=64)
+        for h in range(2):
+            nc.vector.tensor_copy(
+                key_scales[:].rearrange("p (r s) -> p r s", r=PACK)[:, 2 * h : 2 * h + 2, :],
+                spread[:].rearrange("p (s r) -> p r s", r=PACK)[:, 2 * h : 2 * h + 2, :],
+            )
+        grouped1 = sb.tile([P, QC, PACK], BF16, name="q_grouped1", align_bytes=64)
+        round_queries(nc.scalar.copy, grouped1, 1)
+        quantise_queries(1, grouped1)
+        grouped2 = shared.tile([P, QC, PACK], BF16, name="q_grouped2", offset=spread_at, align_bytes=64)
+        round_queries(nc.vector.tensor_copy, grouped2, 2)
         quantise_queries(2, grouped2)
 
         HALF = PACK // 2
@@ -208,10 +204,7 @@ def tile_attend_plw_cap_topk_kernel(tc, qT, k_words, k_scales, ls, offs, out_0, 
             logits[c, r0] = shift(capped[:], c * QC, "log%d%d" % (c, r0))
             if (c, r0) == (0, HALF):
                 grouped3 = sb.tile([P, QC, PACK], BF16, name="q_grouped3", tag="cap00", align_bytes=64)
-                nc.vector.tensor_copy(
-                    grouped3[:].rearrange("p (g i) j -> p g j i", i=4),
-                    q_raw[3][:].rearrange("p j (g i) -> p g j i", i=4),
-                )
+                round_queries(nc.vector.tensor_copy, grouped3, 3)
             if (c, r0) == (1, 0):
                 quantise_queries(3, grouped3)
         bank3 = multiply(3, 0, PACK)

@@ -43,7 +43,7 @@ def tile_attend_plw_cap_topk_kernel(tc, qT, k_words, k_scales, ls, offs, out_0, 
 
         offsets = sb.tile([P, N // 16], U16, name="offsets")
         nc.sync.dma_start(offsets[:], offs)
-        pool_words = shared.tile([P, T], U32, name="pool_words", offset=0, align_bytes=64)
+        pool_words = shared.tile([P, T], U32, name="pool_words", offset=0, align_bytes=256)
         nc.sync.dma_start(
             pool_words[:].bitcast(I32),
             k_words[0].rearrange("p t r -> p (t r)").bitcast(I32),
@@ -61,7 +61,7 @@ def tile_attend_plw_cap_topk_kernel(tc, qT, k_words, k_scales, ls, offs, out_0, 
             nc.sync.dma_start(tile[:], q_rows[:, :, c * QC : (c + 1) * QC])
 
         for c in range(2):
-            load_queries(c, sb.tile([P, PACK, QC], F32, name="q_raw%d" % c))
+            load_queries(c, sb.tile([P, PACK, QC], F32, name="q_raw%d" % c, align_bytes=256))
 
         identity = sb.tile([P, P], F32, name="identity")
         make_identity(nc, identity[:])
@@ -112,11 +112,8 @@ def tile_attend_plw_cap_topk_kernel(tc, qT, k_words, k_scales, ls, offs, out_0, 
         round_queries(nc.scalar.copy, grouped0, 0)
         quantise_queries(0, grouped0)
         key_scales = shared.tile([P, N], U8, name="key_scales", offset=early + 2 * QC, align_bytes=64)
-        for h in range(2):
-            nc.vector.tensor_copy(
-                key_scales[:].rearrange("p (r s) -> p r s", r=PACK)[:, 2 * h : 2 * h + 2, :],
-                spread[:].rearrange("p (s r) -> p r s", r=PACK)[:, 2 * h : 2 * h + 2, :],
-            )
+        for r in range(PACK):
+            nc.vector.tensor_copy(key_scales[:, r * P : (r + 1) * P], spread[:, r:N:PACK])
         grouped1 = sb.tile([P, QC, PACK], BF16, name="q_grouped1", align_bytes=64)
         round_queries(nc.scalar.copy, grouped1, 1)
         quantise_queries(1, grouped1)
@@ -144,7 +141,7 @@ def tile_attend_plw_cap_topk_kernel(tc, qT, k_words, k_scales, ls, offs, out_0, 
         y_rows = out_0.rearrange("(p r) q -> p r q", r=PACK)
         words_out = out_1[0].rearrange("p q u -> p (q u)").bitcast(I32)
         y_grouped = sb.tile([P, NQ * PACK], BF16, name="y_grouped", align_bytes=64)
-        y = [sb.tile([P, PACK, QC], F32, name="y%d" % c) for c in range(CHUNKS)]
+        y = [sb.tile([P, PACK, QC], F32, name="y%d" % c, align_bytes=256) for c in range(CHUNKS)]
 
         def staging(shape, name, tag):
             return sb.tile(shape, F32, name=name, tag=tag, align_bytes=64)
@@ -216,11 +213,12 @@ def tile_attend_plw_cap_topk_kernel(tc, qT, k_words, k_scales, ls, offs, out_0, 
         cap(capped2[:], bank2[:])
         group(0, QC)
         logits[2] = shift(capped2[:], 2 * QC, "log2")
-        first_words = sb.tile([P, 2 * QC], U32, name="first_words", align_bytes=64)
+        first_words = sb.tile([P, QC], U32, name="first_words", align_bytes=256)
         planes(first_words, 0, 0, QC)
         for r0 in (0, HALF):
             weigh(y[1][:, r0 : r0 + HALF, :], logits[1, r0][:])
             store(1, r0, HALF)
+        nc.sync.dma_start(words_out[:, 0:QC], first_words[:].bitcast(I32))
         parts = [slice(0, tail), slice(tail, QC)]
         capped3 = [staging([P, PACK, tail], "capped3%d" % h, "log1%d" % (h * HALF)) for h in range(2)]
         for h in range(2):
@@ -230,8 +228,8 @@ def tile_attend_plw_cap_topk_kernel(tc, qT, k_words, k_scales, ls, offs, out_0, 
         for r0 in (0, HALF):
             weigh(y[2][:, r0 : r0 + HALF, :], logits[2][:, r0 : r0 + HALF, :])
             store(2, r0, HALF)
-        planes(first_words, QC, QC, QC)
-        nc.sync.dma_start(words_out[:, 0 : 2 * QC], first_words[:].bitcast(I32))
+        later_words = sb.tile([P, NQ - QC], U32, name="later_words", align_bytes=256)
+        planes(later_words, 0, QC, QC)
         group(2 * QC, QC)
         weigh(y[3][:, :, parts[0]], logit3[0][:])
         group(3 * QC, tail)
@@ -242,10 +240,9 @@ def tile_attend_plw_cap_topk_kernel(tc, qT, k_words, k_scales, ls, offs, out_0, 
         for r0 in (0, HALF):
             weigh(y[3][:, r0 : r0 + HALF, parts[1]], logit3[1][:, r0 : r0 + HALF, :])
             store(3, r0, HALF)
-        later_words = sb.tile([P, 2 * QC], U32, name="later_words", align_bytes=64)
-        planes(later_words, 0, 2 * QC, QC)
-        planes(later_words, QC, 3 * QC, QC)
-        nc.sync.dma_start(words_out[:, 2 * QC : NQ], later_words[:].bitcast(I32))
+        planes(later_words, QC, 2 * QC, QC)
+        planes(later_words, 2 * QC, 3 * QC, QC)
+        nc.sync.dma_start(words_out[:, QC:NQ], later_words[:].bitcast(I32))
         for j in range(4):
             queue = nc.sync if j == 3 else nc.scalar
             queue.dma_start(out_2[0, j:16:4, :].bitcast(I32), y_scales[j:P:32, :].bitcast(I32))

@@ -233,13 +233,14 @@ def tile_attend_plw_cap_topk_kernel(tc, qT, k_words, k_scales, ls, offs, out_0, 
         group(2 * QC, QC)
         weigh(y[3][:, :, parts[0]], logit3[0][:])
         group(3 * QC, tail)
+        weigh(y[3][:, 0:HALF, parts[1]], logit3[1][:, 0:HALF, :])
+        store(3, 0, HALF)
         weigh(
             group_cols(3 * QC + tail, tail).rearrange("p (q r) -> p q r", r=PACK),
             logit3[1][:].rearrange("p r q -> p q r"),
         )
-        for r0 in (0, HALF):
-            weigh(y[3][:, r0 : r0 + HALF, parts[1]], logit3[1][:, r0 : r0 + HALF, :])
-            store(3, r0, HALF)
+        weigh(y[3][:, HALF:PACK, parts[1]], logit3[1][:, HALF:PACK, :])
+        store(3, HALF, HALF)
         planes(later_words, QC, 2 * QC, QC)
         planes(later_words, 2 * QC, 3 * QC, QC)
         nc.sync.dma_start(words_out[:, QC:NQ], later_words[:].bitcast(I32))

from contextlib import ExitStack

import concourse.mybir as mybir
from concourse.masks import make_identity

N, T, D, NQ = 512, 2048, 512, 512
FLOPS = 2 * N * D * NQ

F32 = mybir.dt.float32
BF16 = mybir.dt.bfloat16
I32 = mybir.dt.int32
U32 = mybir.dt.uint32
U16 = mybir.dt.uint16
U8 = mybir.dt.uint8
FP8X4 = mybir.dt.float8_e4m3fn_x4
ACT = mybir.ActivationFunctionType
ALU = mybir.AluOpType

P = 128
PACK = 4
QC = 128
CHUNKS = NQ // QC
CAP = 20.0


def tile_attend_plw_cap_topk_kernel(tc, qT, k_words, k_scales, ls, offs, out_0, out_1, out_2):
    nc = tc.nc
    with ExitStack() as ctx:
        sb = ctx.enter_context(tc.tile_pool(name="sb", bufs=1))
        shared = ctx.enter_context(tc.tile_pool(name="shared", bufs=1))
        ps = ctx.enter_context(tc.psum_pool(name="ps", bufs=1))

        raw_bytes = 4 * PACK * QC
        late = 4 * T
        early = late + 2 * raw_bytes
        spread_at = early + 2 * QC + N + 4 * QC

        pool_scales = shared.tile([P, T], U8, name="pool_scales", offset=late + raw_bytes // 2, align_bytes=64)
        nc.scalar.dma_start(pool_scales[P - 16 : P, :].bitcast(I32), k_scales[0].bitcast(I32))
        nc.vector.memset(pool_scales[0 : P - 16, :].bitcast(I32), 0)
        spread = sb.tile([P, N], U8, name="spread", align_bytes=64)
        nc.vector.memset(spread[:].bitcast(I32), 0)

        offsets = sb.tile([P, N // 16], U16, name="offsets")
        nc.sync.dma_start(offsets[:], offs)
        pool_words = shared.tile([P, T], U32, name="pool_words", offset=0, align_bytes=256)
        nc.sync.dma_start(
            pool_words[:].bitcast(I32),
            k_words[0].rearrange("p t r -> p (t r)").bitcast(I32),
        )
        ls_cols = sb.tile([P, PACK], F32, name="ls_cols")
        nc.sync.dma_start(ls_cols[:], ls[0, 0, :].rearrange("(n m) -> n m", m=PACK))
        minus_ls = shared.tile([P, 80], F32, name="minus_ls", offset=early, align_bytes=64)
        nc.scalar.activation(minus_ls[:, 0:PACK], ls_cols[:], ACT.Copy, scale=-1.0 / CAP)

        q_rows = qT[0].rearrange("(p j) q -> p j q", j=PACK)
        q_raw = {}

        def load_queries(c, tile):
            q_raw[c] = tile
            nc.sync.dma_start(tile[:], q_rows[:, :, c * QC : (c + 1) * QC])

        for c in range(2):
            load_queries(c, sb.tile([P, PACK, QC], F32, name="q_raw%d" % c, align_bytes=256))

        identity = sb.tile([P, P], F32, name="identity")
        make_identity(nc, identity[:])

        listed_scales = shared.tile([P, N], U8, name="listed_scales", offset=spread_at - N // 2, align_bytes=64)
        nc.vector.tensor_copy(listed_scales[:], pool_scales[:].indirect(offsets[:]))
        for j in range(4):
            nc.sync.dma_start(spread[j:P:32, :].bitcast(I32), listed_scales[P - 16 + j : P : 4, :].bitcast(I32))
        for c in range(2, CHUNKS):
            load_queries(
                c, shared.tile([P, PACK, QC], F32, name="q_raw%d" % c, offset=late + raw_bytes * (c - 2), align_bytes=64)
            )

        ls_bank = ps.tile([P, NQ], F32, name="ls_bank")
        ls_slots = ls_bank[:].rearrange("p (m n) -> p m n", m=PACK)
        for m in range(PACK):
            nc.tensor.transpose(ls_slots[:, m, :], minus_ls[:, m : m + 1].to_broadcast([P, P]), identity[:])

        key_words = sb.tile([P, N], U32, name="key_words", align_bytes=64)
        nc.vector.tensor_copy(
            key_words[:].rearrange("p (r s) -> p s r", r=PACK),
            pool_words[:].indirect(offsets[:]),
        )

        q_words, q_scales = {}, {}

        def round_queries(copy, grouped, c):
            copy(
                grouped[:].rearrange("p (g i) j -> p g j i", i=4),
                q_raw[c][:].rearrange("p j (g i) -> p g j i", i=4),
            )

        def quantise_queries(c, grouped):
            if c == 0:
                words = shared.tile([P, QC], U32, name="q_words0", offset=0, align_bytes=64)
            elif c == 1:
                words = shared.tile([P, QC], U32, name="q_words1", offset=spread_at - 4 * QC, align_bytes=64)
            else:
                words = sb.tile([P, QC], U32, name="q_words%d" % c, tag="cap02" if c == 3 else "", align_bytes=64)
            if c < 2:
                scales = shared.tile([P, QC], U8, name="q_scales%d" % c, offset=early + c * QC, align_bytes=64)
            else:
                scales = sb.tile([P, QC], U8, name="q_scales%d" % c, align_bytes=64)
            nc.vector.quantize_mx(words[:].bitcast(FP8X4), scales[:], grouped[:].rearrange("p q j -> p (q j)"))
            q_words[c], q_scales[c] = words[:], scales[:]

        grouped0 = sb.tile([P, QC, PACK], BF16, name="q_grouped0", align_bytes=64)
        round_queries(nc.scalar.copy, grouped0, 0)
        quantise_queries(0, grouped0)
        key_scales = shared.tile([P, N], U8, name="key_scales", offset=early + 2 * QC, align_bytes=64)
        for r in range(PACK):
            nc.vector.tensor_copy(key_scales[:, r * P : (r + 1) * P], spread[:, r:N:PACK])
        grouped1 = sb.tile([P, QC, PACK], BF16, name="q_grouped1", align_bytes=64)
        round_queries(nc.scalar.copy, grouped1, 1)
        quantise_queries(1, grouped1)
        grouped2 = shared.tile([P, QC, PACK], BF16, name="q_grouped2", offset=spread_at, align_bytes=64)
        round_queries(nc.vector.tensor_copy, grouped2, 2)
        quantise_queries(2, grouped2)

        HALF = PACK // 2

        def multiply(c, r0, places):
            bank = ps.tile([P, places, QC], F32, name="scores%d_%d" % (c, r0))
            for r in range(r0, r0 + places):
                nc.tensor.matmul_mx(
                    out=bank[:, r - r0, :],
                    lhsT=key_words[:, r * P : (r + 1) * P].bitcast(FP8X4),
                    lhsT_scale=key_scales[:, r * P : (r + 1) * P],
                    rhs=q_words[c].bitcast(FP8X4),
                    rhs_scale=q_scales[c],
                    start=True,
                    stop=True,
                )
            return bank

        y_scales = sb.tile([P, NQ], U8, name="y_scales", align_bytes=64)
        y_rows = out_0.rearrange("(p r) q -> p r q", r=PACK)
        words_out = out_1[0].rearrange("p q u -> p (q u)").bitcast(I32)
        y_grouped = sb.tile([P, NQ * PACK], BF16, name="y_grouped", align_bytes=64)
        y = [sb.tile([P, PACK, QC], F32, name="y%d" % c, align_bytes=256) for c in range(CHUNKS)]

        def staging(shape, name, tag):
            return sb.tile(shape, F32, name=name, tag=tag, align_bytes=64)

        def cap(out, in_):
            nc.scalar.activation(out, in_, ACT.Tanh, scale=1.0 / CAP)

        def add_ls(logit, capped, first):
            places, width = capped.shape[1], capped.shape[2]
            by_query = ls_slots.rearrange("p m n -> p n m")[:, first // PACK : (first + width) // PACK, :]
            nc.vector.tensor_tensor(
                logit.rearrange("p r (n m) -> p r n m", m=PACK),
                capped.rearrange("p r (n m) -> p r n m", m=PACK),
                by_query.unsqueeze(1).to_broadcast([P, places, width // PACK, PACK]),
                ALU.add,
            )

        def shift(capped, first, name):
            logit = staging([P, capped.shape[1], capped.shape[2]], name, name)
            add_ls(logit[:], capped, first)
            return logit

        def group_cols(first, width):
            return y_grouped[:, first * PACK : (first + width) * PACK]

        def weigh(out, logit):
            nc.scalar.activation(out, logit, ACT.Exp, scale=CAP)

        def group(first, width):
            c, part = first // QC, slice(first % QC, first % QC + width)
            nc.vector.tensor_copy(
                group_cols(first, width).rearrange("p (g i r) -> p g r i", i=4, r=PACK),
                y[c][:, :, part].rearrange("p r (g i) -> p g r i", i=4),
            )

        def store(c, r0=0, places=PACK):
            rows = slice(r0, r0 + places)
            nc.sync.dma_start(y_rows[:, rows, c * QC : (c + 1) * QC], y[c][:, rows, :])

        def planes(words, at, first, width):
            nc.vector.quantize_mx(
                words[:, at : at + width].bitcast(FP8X4), y_scales[:, first : first + width], group_cols(first, width)
            )

        halves = [(c, r0) for c in range(2) for r0 in (0, HALF)]
        opening = [multiply(0, r, 1) for r in range(HALF)]
        banks = {key: multiply(key[0], key[1], HALF) for key in halves[1:]}
        bank2 = multiply(2, 0, PACK)
        logits = {}
        for c, r0 in halves:
            capped = staging([P, HALF, QC], "capped%d%d" % (c, r0), "cap%d%d" % (c, r0))
            if (c, r0) == (0, 0):
                for r in range(HALF):
                    cap(capped[:, r : r + 1, :], opening[r][:])
            else:
                cap(capped[:], banks[c, r0][:])
            logits[c, r0] = shift(capped[:], c * QC, "log%d%d" % (c, r0))
            if (c, r0) == (0, HALF):
                grouped3 = sb.tile([P, QC, PACK], BF16, name="q_grouped3", tag="cap00", align_bytes=64)
                round_queries(nc.vector.tensor_copy, grouped3, 3)
            if (c, r0) == (1, 0):
                quantise_queries(3, grouped3)
        bank3 = multiply(3, 0, PACK)
        tail = QC // 2
        for r0 in (0, HALF):
            weigh(y[0][:, r0 : r0 + HALF, :], logits[0, r0][:])
        store(0)
        capped2 = staging([P, PACK, QC], "capped2", "log00")
        cap(capped2[:], bank2[:])
        group(0, QC)
        logits[2] = shift(capped2[:], 2 * QC, "log2")
        first_words = sb.tile([P, QC], U32, name="first_words", align_bytes=256)
        planes(first_words, 0, 0, QC)
        for r0 in (0, HALF):
            weigh(y[1][:, r0 : r0 + HALF, :], logits[1, r0][:])
            store(1, r0, HALF)
        nc.sync.dma_start(words_out[:, 0:QC], first_words[:].bitcast(I32))
        parts = [slice(0, tail), slice(tail, QC)]
        capped3 = [staging([P, PACK, tail], "capped3%d" % h, "log1%d" % (h * HALF)) for h in range(2)]
        for h in range(2):
            cap(capped3[h][:], bank3[:, :, parts[h]])
        group(QC, QC)
        logit3 = [shift(capped3[h][:], 3 * QC + h * tail, "log3%d" % h) for h in range(2)]
        for r0 in (0, HALF):
            weigh(y[2][:, r0 : r0 + HALF, :], logits[2][:, r0 : r0 + HALF, :])
            store(2, r0, HALF)
        later_words = sb.tile([P, NQ - QC], U32, name="later_words", align_bytes=256)
        planes(later_words, 0, QC, QC)
        group(2 * QC, QC)
        weigh(y[3][:, :, parts[0]], logit3[0][:])
        group(3 * QC, tail)
        weigh(y[3][:, 0:HALF, parts[1]], logit3[1][:, 0:HALF, :])
        store(3, 0, HALF)
        weigh(
            group_cols(3 * QC + tail, tail).rearrange("p (q r) -> p q r", r=PACK),
            logit3[1][:].rearrange("p r q -> p q r"),
        )
        weigh(y[3][:, HALF:PACK, parts[1]], logit3[1][:, HALF:PACK, :])
        store(3, HALF, HALF)
        planes(later_words, QC, 2 * QC, QC)
        planes(later_words, 2 * QC, 3 * QC, QC)
        nc.sync.dma_start(words_out[:, QC:NQ], later_words[:].bitcast(I32))
        for j in range(4):
            queue = nc.sync if j == 3 else nc.scalar
            queue.dma_start(out_2[0, j:16:4, :].bitcast(I32), y_scales[j:P:32, :].bitcast(I32))
